import numpy as np, ml_dtypes
CORES = [40,41,42,43,44,45,46,47]
N = 8
import mx_ref
BF = ml_dtypes.bfloat16
def entries(a):
    return np.ascontiguousarray(a.T).reshape(-1)
def table(e):
    return np.ascontiguousarray(np.reshape(e, (-1, 16)).T).astype(np.int32)
def cut(t, i, w=512):
    return t[:, w * i:w * i + w]
def f(rng, *shape):
    return mx_ref.flush((rng.standard_normal(shape, dtype=np.float32) * np.exp2(rng.integers(-2, 3, shape[:-1] + (1,)))).astype(BF))
def wide(rng, *shape, cols=0):
    v = rng.standard_normal(shape, dtype=np.float32) * np.exp2(rng.integers(-12, 13, shape)).astype(np.float32)
    if cols: v *= np.repeat(np.exp2(rng.integers(-cols, cols + 1, shape[:-2] + (1, shape[-1] // 4))) * (rng.random(shape[:-2] + (1, shape[-1] // 4)) > 0.0625), 4, axis=-1).astype(np.float32)
    return mx_ref.flush(v.astype(BF))
T, S, CAPP, O = 512, 512, 128, 4
def counts(rng, zero=0.125, quiet=()):
    send = [r for r in range(N) if r not in quiet]
    n = np.zeros((N, N), int)
    for d in range(N): n[send[rng.integers(0, len(send))], d] = 16
    for k in rng.permutation(N * N):
        r, d = k // N, k % N
        if r in send and rng.random() > zero: n[r, d] += min(rng.integers(0, CAPP + 1), CAPP - n[r, d], T - n[r].sum(), S - n[:, d].sum())
    return n
def stored(n):
    return np.stack([table(np.concatenate([n[r], np.zeros(16 - N, int)])) for r in range(N)])
def setup_inputs(rng):
    return {"x": f(rng, N, 128, 4 * T), "cn": stored(counts(rng)), "w": f(rng, N, 128, 512 * O)}
def setup_inputs_full(rng):
    n = np.zeros((N, N), int); a, b = rng.permutation(N), rng.permutation(N)
    for i in range(N):
        for j in range(min(T // CAPP, S // CAPP, N)): n[a[i], b[(i + j) % N]] = CAPP
    return {**setup_inputs(rng), "cn": stored(n)}
def setup_inputs_none(rng):
    n = counts(rng, zero=0.6, quiet=(int(rng.integers(0, N)),)); n[:, rng.integers(0, N)] = 0
    return {**setup_inputs(rng), "cn": stored(n)}
def setup_inputs_skew(rng):
    n = rng.integers(0, 4, (N, N)); n[rng.integers(0, N, N), np.arange(N)] = 4
    d = rng.integers(0, N); n[:, d] = 0; n[(d + rng.integers(1, N)) % N, d] = CAPP
    while n[:, d].sum() < S:
        q = rng.integers(0, N)
        if n[q, d] < CAPP: n[q, d] += 1
    return {**setup_inputs(rng), "cn": stored(n)}
def setup_inputs_last(rng):
    n = np.zeros((N, N), int)
    for r in (N - 2, N - 1):
        n[r] = 1
        while n[r].sum() < T:
            q = rng.integers(0, N)
            if n[r, q] < CAPP: n[r, q] += 1
    return {**setup_inputs(rng), "cn": stored(n)}
def setup_inputs_spread(rng):
    d = setup_inputs(rng); d["x"] = wide(rng, N, 128, 4 * T, cols=8); return d
def check_inputs(d):
    b = []
    e = np.stack([entries(d["cn"][r]) for r in range(N)]).astype(np.int64); n = e[:, :N]
    if n.min() < 0 or n.max() > CAPP: b.append("count")
    if (e[:, N:] != 0).any(): b.append("zeros")
    if (n.sum(axis=1) > T).any(): b.append("sent")
    if (n.sum(axis=0) > S).any(): b.append("received")
    return b
def reference(x, cn, w):
    n = np.stack([entries(cn[r])[:N] for r in range(N)])
    y = np.zeros((N, 128, O * S), np.float32); ln = np.zeros((N, 1, N + 1), np.float32)
    for d in range(N):
        ln[d, 0, 1:] = np.add.accumulate(n[:, d])
        k = int(np.add.reduce(n[:, d])); t = np.zeros((128, 4 * S), BF); at = 0
        for s in range(N):
            a, m = int(np.add.reduce(n[s, :d])), int(n[s, d])
            t[:, 4 * at:4 * (at + m)] = x[s][:, 4 * a:4 * (a + m)]; at += m
        q = mx_ref.quantize(t)
        for o in range(O): y[d][:, S * o:S * o + k] = mx_ref.matmul(mx_ref.quantize(np.ascontiguousarray(cut(w[d], o))), q)[:, :k]
    return {"y": y, "ln": ln}

@@ -1,0 +1,301 @@
+from concourse.bass import DstId, RemoteDMATransfer
+from concourse.mybir import dt, AluOpType, ActivationFunctionType
+
+N, T_COLS, CAPP, S_COLS, O = 8, 512, 128, 512, 4
+ZERO = N * CAPP
+PART = 320
+G = N + 1
+SCALE_CALLS = [[0, 1], [2]]
+
+SCRATCH = {
+    "xt": ("sbuf", [128, 4 * T_COLS], "bfloat16"),
+    "wt": ("sbuf", [128, 512 * O], "bfloat16"),
+    "zt": ("sbuf", [128, 512], "bfloat16"),
+    "q": ("sbuf", [128, T_COLS], "float8_e4m3fn_x4"),
+    "qs": ("sbuf", [128, T_COLS], "uint8"),
+    "slot": ("sbuf", [128, N * CAPP], "float8_e4m3fn_x4"),
+    "slots": ("sbuf", [128, N * CAPP], "uint8"),
+    "land": ("sbuf", [128, ZERO + 128], "float8_e4m3fn_x4"),
+    "lands": ("sbuf", [128, ZERO + 128], "uint8"),
+    "wq": ("sbuf", [128, 128 * O], "float8_e4m3fn_x4"),
+    "wqs": ("sbuf", [128, 128 * O], "uint8"),
+    "pk": ("sbuf", [128, S_COLS], "float8_e4m3fn_x4"),
+    "pks": ("sbuf", [128, S_COLS], "uint8"),
+    "yo": ("sbuf", [128, O * S_COLS], "float32"),
+    "ps": ("psum", [128, 512 * 2 * O], "float32"),
+    "cn1": ("sbuf", [128, 16], "int32"),
+    "cnb": ("sbuf", [128, 16], "int32"),
+    "zi": ("sbuf", [128, 16], "int32"),
+    "pi": ("sbuf", [128, 8], "int32"),
+    "pm": ("sbuf", [128, 8], "int32"),
+    "p0": ("sbuf", [128, 8], "float32"),
+    "bi": ("sbuf", [128, 32], "int32"),
+    "base": ("sbuf", [128, 32], "float32"),
+    "inc": ("sbuf", [128, 64], "float32"),
+    "zf": ("sbuf", [128, 64], "float32"),
+    "sc": ("sbuf", [128, 64], "float32"),
+    "so": ("sbuf", [128, 64], "uint16"),
+    "cin": ("dram", [N, 128, 1], "int32"),
+    "cg": ("sbuf", [128, 16], "int32"),
+    "cgb": ("sbuf", [128, 16], "int32"),
+    "cf": ("sbuf", [128, 8], "float32"),
+    "mf": ("sbuf", [128, 8], "float32"),
+    "lb": ("sbuf", [128, 16], "float32"),
+    "keep": ("sbuf", [128, 32 * G], "float32"),
+    "t9": ("sbuf", [128, 32 * G], "float32"),
+    "s9": ("sbuf", [128, 32 * G], "float32"),
+    "ro": ("sbuf", [128, 32], "uint16"),
+}
+SEMAPHORES = (["cn", "x0", "x1", "w", "cgot", "arrc", "arrs", "sent", "pi", "bi", "zt", "zq", "incm", "cg", "cgb",
+               "ch", "zi", "zf", "lb0", "pm", "p0", "base", "bc", "i1", "sc", "so", "q0", "q1", "q2", "ownc", "owns",
+               "wq", "cf", "mf", "lb", "k1", "k0", "t0", "t9", "s9", "ro", "lnst", "yst"]
+              + ["pc%d" % i for i in range(3)] + ["pl%d" % i for i in range(3)]
+              + ["ac%d" % i for i in range(2)] + ["as%d" % i for i in range(2)]
+              + ["m%d" % i for i in range(2 * O)] + ["yv%d" % i for i in range(O)] + ["ys%d" % i for i in range(O)])
+
+
+def groups_of(topo, cores, r):
+    first = [d for d in range(2) if d != r]
+    rest = [d for d in range(2, N) if d != r]
+    near = [d for d in rest if topo.die(cores[d]) == topo.die(cores[r])]
+    far = [d for d in rest if d not in near]
+    return [first, [near[0], far[0]], near[1:] + far[1:]]
+
+
+def engines_for(topo, cores, r, group, scales):
+    e = topo.engines(cores[r], cores[group[0]])
+    if len(group) == 1:
+        return {group[0]: e}
+    fars = [d for d in group if topo.die(cores[d]) != topo.die(cores[r])]
+    nears = [d for d in group if d not in fars]
+    a, b = (e[1::2], e[0::2]) if scales else (e[0::2], e[1::2])
+    h = len(a) // 2
+    if len(group) == 2:
+        cut = [a, b]
+    elif len(group) == 3:
+        cut = [b[:h], b[h:], a] if len(fars) == 2 else [a, b[:h], b[h:]]
+    else:
+        cut = [a[:h], a[h:], b[:h], b[h:]]
+    return {d: c for d, c in zip(fars + nears, cut)}
+
+
+def bits(es):
+    return sum(1 << e for e in es)
+
+
+def runs(group):
+    out = []
+    for d in sorted(group):
+        if out and out[-1][1] == d:
+            out[-1][1] = d + 1
+        else:
+            out.append([d, d + 1])
+    return out
+
+
+def rank_program(g, core, T, topo):
+    r = T.rank_of(core)
+    if r is None:
+        return
+    cores = list(T.cores)
+    others = [s for s in range(N) if s != r]
+    V, A, P, Y, sem = g.vector, g.scalar, g.tensor, g.sync, T.sem
+    copy = ActivationFunctionType.Copy
+    add, mx, mn, mul = AluOpType.add, AluOpType.max, AluOpType.min, AluOpType.mult
+    groups = groups_of(topo, cores, r)
+    sent = [0]
+
+    def dst_id(d):
+        rid, pid, _ = topo.addr(cores[d])
+        return DstId(rid=rid, pnc=pid)
+
+    def send(items, rsem):
+        for it in items:
+            sent[0] += len(it[1])
+        if len(items) == 1:
+            d, es, src, dst = items[0]
+            rid, pid, _ = topo.addr(cores[d])
+            g.remote_dma(out_ap=dst, in_ap=src, remote_sem=rsem, local_sem=sem.sent, pid=pid, routing_id=rid,
+                         dma_engine_mask=bits(es))
+            return
+        g.remote_dma_fused([RemoteDMATransfer(dst_ids=[dst_id(d)], dma_engine_mask=bits(es), remote_sem=rsem,
+                                              srcs=[src], dsts=[dst]) for d, es, src, dst in items],
+                           local_sem=sem.sent)
+
+    h = 2 * T_COLS
+    Y.dma_start(T.cn1[0:1, 0:16], T.cn[:]).then_inc(sem.cn, 16)
+    A.dma_start(T.cin[r, 0:16, :], T.cn[:]).then_inc(sem.ch, 16)
+    V.memset(T.zi[:], 0).then_inc(sem.zi, 1)
+    A.wait_ge(sem.zi, 1)
+    A.dma_start(T.cin[r, 16:128, :], T.zi[0:7, 0:16]).then_inc(sem.ch, 16)
+    Y.wait_ge(sem.zi, 1)
+    Y.dma_start(T.xt[:, 0:h], T.x[:, 0:h]).then_inc(sem.x0, 16)
+    Y.dma_start(T.xt[:, h:2 * h], T.x[:, h:2 * h]).then_inc(sem.x1, 16)
+    Y.dma_start(T.wt[:], T.w[:]).then_inc(sem.w, 16)
+
+    g.iota(T.pi[:, 0:1], [[1, 1]], 0, 1).then_inc(sem.pi, 1)
+    g.iota(T.bi[:], [[16, 32]], 0, 0).then_inc(sem.bi, 1)
+    V.memset(T.inc[:], 16.0).then_inc(sem.incm, 1)
+    V.memset(T.zf[:], 0.0).then_inc(sem.zf, 1)
+    V.wait_ge(sem.pi, 1)
+    V.tensor_scalar(T.pm[:, 0:1], T.pi[:, 0:1], 15, None, AluOpType.bitwise_and).then_inc(sem.pm, 1)
+    V.wait_ge(sem.pm, 1)
+    V.tensor_scalar(T.p0[:, 0:1], T.pm[:, 0:1], -16.0, None, add).then_inc(sem.p0, 1)
+    V.memset(T.lb[:, 0:1], 0.0).then_inc(sem.lb0, 1)
+    V.memset(T.keep[:], 1.0).then_inc(sem.k1, 1)
+    V.memset(T.zt[:], 0.0).then_inc(sem.zt, 1)
+
+    g.wait_ge(sem.cn, 16)
+    g.partition_broadcast(T.cnb[:], T.cn1[0:1, 0:16], 128).then_inc(sem.bc, 1)
+    V.wait_ge(sem.bc, 1)
+    V.wait_ge(sem.incm, 1)
+    V.tensor_scalar(T.inc[:, 8:64:8], T.cnb[:, 0:7], -112.0, None, add).then_inc(sem.i1, 1)
+    V.wait_ge(sem.i1, 1)
+    V.wait_ge(sem.zf, 1)
+    V.wait_ge(sem.p0, 1)
+    V.tensor_tensor_scan(T.sc[:], T.inc[:], T.zf[:], T.p0[:, 0:1], add, mx).then_inc(sem.sc, 1)
+    V.wait_ge(sem.sc, 1)
+    V.tensor_scalar(T.so[:], T.sc[:], float(T_COLS - 1), None, mn).then_inc(sem.so, 1)
+
+    g.wait_ge(sem.ch, 32)
+    g.remote_dma_fused([RemoteDMATransfer(dst_ids=[dst_id(d) for d in others],
+                                          dma_engine_mask=bits(topo.engines(core, cores[others[0]])[0:1]),
+                                          remote_sem=sem.cgot, srcs=[T.cin[r]], dsts=[T.cin[r] for d in others])],
+                       local_sem=sem.sent)
+    sent[0] += 1
+    Y.wait_ge(sem.ch, 32)
+    Y.wait_ge(sem.cgot, len(others))
+    Y.dma_start(T.cg[0:1, 0:16], T.cin[:, r:r + 2, 0]).then_inc(sem.cg, 16)
+
+    V.wait_ge(sem.x0, 16)
+    V.quantize_mx(T.q[:, 0:128], T.qs[:, 0:128], T.xt[:, 0:512]).then_inc(sem.q0, 1)
+    V.quantize_mx(T.q[:, 128:256], T.qs[:, 128:256], T.xt[:, 512:1024]).then_inc(sem.q1, 1)
+    V.wait_ge(sem.so, 1)
+    V.wait_ge(sem.q0, 1)
+    V.wait_ge(sem.q1, 1)
+    A.wait_ge(sem.so, 1)
+    A.wait_ge(sem.q0, 1)
+    A.wait_ge(sem.q1, 1)
+
+    me = slice(128 * r, 128 * r + 128)
+    picks = []
+    for k, group in enumerate(groups):
+        if k == 1:
+            V.wait_ge(sem.bi, 1)
+            V.tensor_scalar(T.base[:], T.bi[:], T.p0[:, 0:1], 16.0, add, add).then_inc(sem.base, 1)
+            V.tensor_scalar(T.t9[:, 0:32 * G:G], T.bi[:], T.p0[:, 0:1], 16.0, add, add).then_inc(sem.t0, 1)
+            V.wait_ge(sem.x1, 16)
+            V.quantize_mx(T.q[:, 256:512], T.qs[:, 256:512], T.xt[:, 1024:2048]).then_inc(sem.q2, 1)
+            V.wait_ge(sem.q2, 1)
+            A.wait_ge(sem.q2, 1)
+        w = 256 if k == 0 else T_COLS
+        rr = runs([d for d in group if d != 0])
+        picks.append(len(rr))
+        for a, b in rr:
+            V.tensor_copy(T.slot[:, 128 * a:128 * b].bitcast(dt.uint32),
+                          T.q[:, 0:w].bitcast(dt.uint32).indirect(T.so[:, 8 * a:8 * b])).then_inc(sem["pc%d" % k], 1)
+            A.activation(T.slots[:, 128 * a:128 * b], T.qs[:, 0:w].indirect(T.so[:, 8 * a:8 * b]),
+                         copy).then_inc(sem["pl%d" % k], 1)
+        if 0 in group:
+            g.wait_ge(sem.q0, 1)
+        if rr:
+            g.wait_ge(sem["pc%d" % k], len(rr))
+        e = engines_for(topo, cores, r, group, False)
+        send([(d, e[d], (T.slot if d else T.q)[:, 128 * d:128 * d + 128].bitcast(dt.uint8),
+               T.land[:, me].bitcast(dt.uint8)) for d in group], sem.arrc)
+        if k == len(groups) - 1:
+            g.wait_ge(sem.cg, 16)
+            g.partition_broadcast(T.cgb[:], T.cg[0:1, 0:16], 128).then_inc(sem.cgb, 1)
+        for ks in SCALE_CALLS:
+            if ks[-1] == k:
+                for j in ks:
+                    if picks[j]:
+                        g.wait_ge(sem["pl%d" % j], picks[j])
+                both = [d for j in ks for d in groups[j]]
+                e = engines_for(topo, cores, r, both, True)
+                send([(d, e[d], (T.slots if d else T.qs)[:, 128 * d:128 * d + 128], T.lands[:, me]) for d in both],
+                     sem.arrs)
+
+    V.tensor_copy(T.land[:, me].bitcast(dt.uint32),
+                  T.q[:].bitcast(dt.uint32).indirect(T.so[:, 8 * r:8 * r + 8])).then_inc(sem.ownc, 1)
+    A.activation(T.lands[:, me], T.qs[:].indirect(T.so[:, 8 * r:8 * r + 8]), copy).then_inc(sem.owns, 1)
+    V.wait_ge(sem.k1, 1)
+    V.memset(T.keep[:, 0:32 * G:G], 0.0).then_inc(sem.k0, 1)
+    V.wait_ge(sem.zt, 1)
+    V.quantize_mx(T.land[:, ZERO:ZERO + 128], T.lands[:, ZERO:ZERO + 128], T.zt[:]).then_inc(sem.zq, 1)
+    V.wait_ge(sem.w, 16)
+    V.quantize_mx(T.wq[:], T.wqs[:], T.wt[:]).then_inc(sem.wq, 1)
+
+    V.wait_ge(sem.cgb, 1)
+    V.tensor_copy(T.cf[:], T.cgb[:, 0:16:2]).then_inc(sem.cf, 1)
+    V.tensor_scalar(T.mf[:], T.cgb[:, 0:16:2], -1.0, float(CAPP), mul, add).then_inc(sem.mf, 1)
+    V.wait_ge(sem.cf, 1)
+    V.tensor_tensor_scan(T.lb[:, 1:9], T.cf[:], T.cf[:], 0.0, add, mx).then_inc(sem.lb, 1)
+    V.wait_ge(sem.base, 1)
+    V.wait_ge(sem.mf, 1)
+    V.wait_ge(sem.lb, 1)
+    for s in range(N):
+        V.tensor_scalar(T.t9[:, s + 1:32 * G:G], T.base[:], T.lb[:, s + 1:s + 2], T.mf[:, s:s + 1],
+                        AluOpType.is_ge, mul).then_inc(sem.t9, 1)
+    V.wait_ge(sem.k0, 1)
+    V.wait_ge(sem.t0, 1)
+    V.wait_ge(sem.t9, N)
+    V.tensor_tensor_scan(T.s9[:], T.keep[:], T.t9[:], 0.0, mul, add).then_inc(sem.s9, 1)
+    V.wait_ge(sem.s9, 1)
+    V.tensor_scalar(T.ro[:], T.s9[:, N:32 * G:G], float(ZERO), None, mn).then_inc(sem.ro, 1)
+    Y.wait_ge(sem.lb0, 1)
+    Y.wait_ge(sem.lb, 1)
+    Y.dma_start(T.ln[:], T.lb[0:1, 0:9]).then_inc(sem.lnst, 16)
+
+    nc = ns = 0
+    for s in others:
+        gs = groups_of(topo, cores, s)
+        for group in gs:
+            if r in group:
+                nc += len(engines_for(topo, cores, s, group, False)[r])
+        for ks in SCALE_CALLS:
+            both = [d for j in ks for d in gs[j]]
+            if r in both:
+                ns += len(engines_for(topo, cores, s, both, True)[r])
+    for q in (V, A):
+        q.wait_ge(sem.ro, 1)
+        q.wait_ge(sem.zq, 1)
+    V.wait_ge(sem.ownc, 1)
+    A.wait_ge(sem.owns, 1)
+    V.wait_ge(sem.arrc, nc)
+    A.wait_ge(sem.arrs, ns)
+    parts = [(0, PART), (PART, S_COLS)]
+    for i, (a, b) in enumerate(parts):
+        V.tensor_copy(T.pk[:, a:b].bitcast(dt.uint32),
+                      T.land[:].bitcast(dt.uint32).indirect(T.ro[:, a // 16:b // 16])).then_inc(sem["ac%d" % i], 1)
+        A.activation(T.pks[:, a:b], T.lands[:].indirect(T.ro[:, a // 16:b // 16]), copy).then_inc(sem["as%d" % i], 1)
+
+    P.wait_ge(sem.wq, 1)
+    for o in range(O):
+        for i, (a, b) in enumerate(parts):
+            if o == 0:
+                P.wait_ge(sem["ac%d" % i], 1)
+                P.wait_ge(sem["as%d" % i], 1)
+            k = 2 * o + i
+            P.matmul_mx(T.ps[:, 512 * k:512 * k + b - a], T.wq[:, 128 * o:128 * o + 128],
+                        T.wqs[:, 128 * o:128 * o + 128], T.pk[:, a:b], T.pks[:, a:b], True,
+                        True).then_inc(sem["m%d" % k], 1)
+    stores = 0
+    for o in range(O):
+        at = S_COLS * o
+        V.wait_ge(sem["m%d" % (2 * o)], 1)
+        V.tensor_copy(T.yo[:, at:at + PART], T.ps[:, 1024 * o:1024 * o + PART]).then_inc(sem["yv%d" % o], 1)
+        A.wait_ge(sem["m%d" % (2 * o + 1)], 1)
+        A.activation(T.yo[:, at + PART:at + S_COLS], T.ps[:, 1024 * o + 512:1024 * o + 512 + S_COLS - PART],
+                     copy).then_inc(sem["ys%d" % o], 1)
+        cuts = [0, PART, S_COLS] if o == 0 else [0, S_COLS]
+        Y.wait_ge(sem["yv%d" % o], 1)
+        for a, b in zip(cuts, cuts[1:]):
+            if b == S_COLS:
+                Y.wait_ge(sem["ys%d" % o], 1)
+            Y.dma_start(T.y[:, at + a:at + b], T.yo[:, at + a:at + b]).then_inc(sem.yst, 16)
+            stores += 1
+
+    Y.wait_ge(sem.lnst, 16)
+    Y.wait_ge(sem.yst, 16 * stores)
+    g.wait_ge(sem.sent, sent[0])

@@ -3,9 +3,12 @@ from concourse.mybir import dt, AluOpType, ActivationFunctionType
 
 N, T_COLS, CAPP, S_COLS, O = 8, 512, 128, 512, 4
 ZERO = N * CAPP
-PART = 320
+PART = 256
 G = N + 1
-SCALE_CALLS = [[0, 1], [2]]
+X_CUTS = [0, 256, 384, 512]
+EARLY = 3
+W_CUTS = [0, 1, 2, 4]
+BIG = 4096
 
 SCRATCH = {
     "xt": ("sbuf", [128, 4 * T_COLS], "bfloat16"),
@@ -24,48 +27,46 @@ SCRATCH = {
     "yo": ("sbuf", [128, O * S_COLS], "float32"),
     "ps": ("psum", [128, 512 * 2 * O], "float32"),
     "cn1": ("sbuf", [128, 16], "int32"),
-    "cnb": ("sbuf", [128, 16], "int32"),
-    "zi": ("sbuf", [128, 16], "int32"),
+    "cnb": ("sbuf", [128, 8], "int32"),
     "pi": ("sbuf", [128, 8], "int32"),
     "pm": ("sbuf", [128, 8], "int32"),
     "p0": ("sbuf", [128, 8], "float32"),
     "bi": ("sbuf", [128, 32], "int32"),
-    "base": ("sbuf", [128, 32], "float32"),
     "inc": ("sbuf", [128, 64], "float32"),
-    "zf": ("sbuf", [128, 64], "float32"),
     "sc": ("sbuf", [128, 64], "float32"),
     "so": ("sbuf", [128, 64], "uint16"),
-    "cin": ("dram", [N, 128, 1], "int32"),
-    "cg": ("sbuf", [128, 16], "int32"),
-    "cgb": ("sbuf", [128, 16], "int32"),
+    "cg": ("sbuf", [128, 4 * N], "int32"),
     "cf": ("sbuf", [128, 8], "float32"),
     "mf": ("sbuf", [128, 8], "float32"),
     "lb": ("sbuf", [128, 16], "float32"),
-    "keep": ("sbuf", [128, 32 * G], "float32"),
-    "t9": ("sbuf", [128, 32 * G], "float32"),
-    "s9": ("sbuf", [128, 32 * G], "float32"),
+    "keep": ("sbuf", [128, 32 * G], "bfloat16"),
+    "t9": ("sbuf", [128, 32 * G], "float16"),
+    "s9": ("sbuf", [128, 32 * G], "float16"),
     "ro": ("sbuf", [128, 32], "uint16"),
 }
-SEMAPHORES = (["cn", "x0", "x1", "w", "cgot", "arrc", "arrs", "sent", "pi", "bi", "zt", "zq", "incm", "cg", "cgb",
-               "ch", "zi", "zf", "lb0", "pm", "p0", "base", "bc", "i1", "sc", "so", "q0", "q1", "q2", "ownc", "owns",
-               "wq", "cf", "mf", "lb", "k1", "k0", "t0", "t9", "s9", "ro", "lnst", "yst"]
+SEMAPHORES = (["cn", "cgot", "arrc", "arrs", "sent", "pi", "bi", "zt", "zq", "incm", "cown", "wgo",
+               "lb0", "pm", "p0", "bc", "i1", "sc", "so", "ownc", "owns",
+               "cf", "mf", "lb", "k1", "k0", "t0", "t9", "s9", "ro", "lnst", "yst"]
+              + ["x%d" % i for i in range(3)] + ["q%d" % i for i in range(3)]
+              + ["w%d" % i for i in range(3)] + ["wq%d" % i for i in range(3)]
               + ["pc%d" % i for i in range(3)] + ["pl%d" % i for i in range(3)]
               + ["ac%d" % i for i in range(2)] + ["as%d" % i for i in range(2)]
-              + ["m%d" % i for i in range(2 * O)] + ["yv%d" % i for i in range(O)] + ["ys%d" % i for i in range(O)])
+              + ["m%d" % i for i in range(2 * O)] + ["y%d" % i for i in range(2 * O)])
 
 
 def groups_of(topo, cores, r):
-    first = [d for d in range(2) if d != r]
-    rest = [d for d in range(2, N) if d != r]
+    early = [d for d in range(EARLY) if d != r]
+    rest = [d for d in range(EARLY, N) if d != r]
     near = [d for d in rest if topo.die(cores[d]) == topo.die(cores[r])]
     far = [d for d in rest if d not in near]
-    return [first, [near[0], far[0]], near[1:] + far[1:]]
+    if len(far) > 2 and r % 2:
+        far = far[2:] + far[:2]
+    late = far + near
+    return [early, late[:2], late[2:]]
 
 
 def engines_for(topo, cores, r, group, scales):
     e = topo.engines(cores[r], cores[group[0]])
-    if len(group) == 1:
-        return {group[0]: e}
     fars = [d for d in group if topo.die(cores[d]) != topo.die(cores[r])]
     nears = [d for d in group if d not in fars]
     a, b = (e[1::2], e[0::2]) if scales else (e[0::2], e[1::2])
@@ -74,9 +75,25 @@ def engines_for(topo, cores, r, group, scales):
         cut = [a, b]
     elif len(group) == 3:
         cut = [b[:h], b[h:], a] if len(fars) == 2 else [a, b[:h], b[h:]]
-    else:
+    elif len(group) == 4:
         cut = [a[:h], a[h:], b[:h], b[h:]]
+    elif len(group) == 5:
+        cut = [a[:h], a[h:], b[:h], b[h:h + h // 2], b[h + h // 2:]]
+    else:
+        cut = [a[i:i + 2] for i in range(0, len(a), 2)] + [b[0:2], b[2:4], b[4:]]
     return {d: c for d, c in zip(fars + nears, cut)}
+
+
+def count_engines(topo, cores, r):
+    others = [d for d in range(N) if d != r]
+    e = topo.engines(cores[r], cores[others[0]])
+    return {d: (e[2 * i + 2:2 * i + 4] if i else e[0:4]) for i, d in enumerate(others)}
+
+
+def calls_of(topo, cores, r):
+    gs = groups_of(topo, cores, r)
+    order = [(False, [0]), (True, [0]), (False, [1]), (True, [1, 2]), (False, [2])]
+    return [(sc, ks, engines_for(topo, cores, r, [d for k in ks for d in gs[k]], sc)) for sc, ks in order]
 
 
 def bits(es):
@@ -105,158 +122,140 @@ def rank_program(g, core, T, topo):
     groups = groups_of(topo, cores, r)
     sent = [0]
 
-    def dst_id(d):
-        rid, pid, _ = topo.addr(cores[d])
-        return DstId(rid=rid, pnc=pid)
-
     def send(items, rsem):
-        for it in items:
-            sent[0] += len(it[1])
-        if len(items) == 1:
-            d, es, src, dst = items[0]
+        out = []
+        for d, es, src, dst in items:
             rid, pid, _ = topo.addr(cores[d])
-            g.remote_dma(out_ap=dst, in_ap=src, remote_sem=rsem, local_sem=sem.sent, pid=pid, routing_id=rid,
-                         dma_engine_mask=bits(es))
-            return
-        g.remote_dma_fused([RemoteDMATransfer(dst_ids=[dst_id(d)], dma_engine_mask=bits(es), remote_sem=rsem,
-                                              srcs=[src], dsts=[dst]) for d, es, src, dst in items],
-                           local_sem=sem.sent)
+            sent[0] += len(es)
+            out.append(RemoteDMATransfer(dst_ids=[DstId(rid=rid, pnc=pid)], dma_engine_mask=bits(es), remote_sem=rsem,
+                                         srcs=[src], dsts=[dst]))
+        g.remote_dma_fused(out, local_sem=sem.sent)
 
-    h = 2 * T_COLS
+    def load_w(k):
+        a, b = 512 * W_CUTS[k], 512 * W_CUTS[k + 1]
+        Y.dma_start(T.wt[:, a:b], T.w[:, a:b]).then_inc(sem["w%d" % k], 16)
+
+    def quantise_w(k):
+        a, b = W_CUTS[k], W_CUTS[k + 1]
+        V.wait_ge(sem["w%d" % k], 16)
+        V.quantize_mx(T.wq[:, 128 * a:128 * b], T.wqs[:, 128 * a:128 * b],
+                      T.wt[:, 512 * a:512 * b]).then_inc(sem["wq%d" % k], 1)
+
     Y.dma_start(T.cn1[0:1, 0:16], T.cn[:]).then_inc(sem.cn, 16)
-    A.dma_start(T.cin[r, 0:16, :], T.cn[:]).then_inc(sem.ch, 16)
-    V.memset(T.zi[:], 0).then_inc(sem.zi, 1)
-    A.wait_ge(sem.zi, 1)
-    A.dma_start(T.cin[r, 16:128, :], T.zi[0:7, 0:16]).then_inc(sem.ch, 16)
-    Y.wait_ge(sem.zi, 1)
-    Y.dma_start(T.xt[:, 0:h], T.x[:, 0:h]).then_inc(sem.x0, 16)
-    Y.dma_start(T.xt[:, h:2 * h], T.x[:, h:2 * h]).then_inc(sem.x1, 16)
-    Y.dma_start(T.wt[:], T.w[:]).then_inc(sem.w, 16)
+    for k, (a, b) in enumerate(zip(X_CUTS, X_CUTS[1:])):
+        Y.dma_start(T.xt[:, 4 * a:4 * b], T.x[:, 4 * a:4 * b]).then_inc(sem["x%d" % k], 16)
+    load_w(0)
 
     g.iota(T.pi[:, 0:1], [[1, 1]], 0, 1).then_inc(sem.pi, 1)
     g.iota(T.bi[:], [[16, 32]], 0, 0).then_inc(sem.bi, 1)
+    V.memset(T.zt[:], 0.0).then_inc(sem.zt, 1)
     V.memset(T.inc[:], 16.0).then_inc(sem.incm, 1)
-    V.memset(T.zf[:], 0.0).then_inc(sem.zf, 1)
+    V.memset(T.keep[:], 1.0).then_inc(sem.k1, 1)
     V.wait_ge(sem.pi, 1)
     V.tensor_scalar(T.pm[:, 0:1], T.pi[:, 0:1], 15, None, AluOpType.bitwise_and).then_inc(sem.pm, 1)
+    V.memset(T.lb[:, 0:1], 0.0).then_inc(sem.lb0, 1)
     V.wait_ge(sem.pm, 1)
     V.tensor_scalar(T.p0[:, 0:1], T.pm[:, 0:1], -16.0, None, add).then_inc(sem.p0, 1)
-    V.memset(T.lb[:, 0:1], 0.0).then_inc(sem.lb0, 1)
-    V.memset(T.keep[:], 1.0).then_inc(sem.k1, 1)
-    V.memset(T.zt[:], 0.0).then_inc(sem.zt, 1)
+    V.wait_ge(sem.k1, 1)
+    V.memset(T.keep[:, 0:32 * G:G], 0.0).then_inc(sem.k0, 1)
+    V.wait_ge(sem.bi, 1)
+    V.wait_ge(sem.p0, 1)
+    V.tensor_scalar(T.t9[:, 0:32 * G:G], T.bi[:], T.p0[:, 0:1], 16.0, add, add).then_inc(sem.t0, 1)
+    V.wait_ge(sem.zt, 1)
+    V.quantize_mx(T.land[:, ZERO:ZERO + 128], T.lands[:, ZERO:ZERO + 128], T.zt[:]).then_inc(sem.zq, 1)
 
     g.wait_ge(sem.cn, 16)
-    g.partition_broadcast(T.cnb[:], T.cn1[0:1, 0:16], 128).then_inc(sem.bc, 1)
+    g.partition_broadcast(T.cnb[:], T.cn1[0:1, 0:8], 128).then_inc(sem.bc, 1)
+    g.wait_ge(sem.bc, 1)
+    e = count_engines(topo, cores, r)
+    send([(d, e[d], T.cnb[:, d:d + 1], T.cg[:, 4 * r:4 * r + 1]) for d in others], sem.cgot)
+
     V.wait_ge(sem.bc, 1)
     V.wait_ge(sem.incm, 1)
     V.tensor_scalar(T.inc[:, 8:64:8], T.cnb[:, 0:7], -112.0, None, add).then_inc(sem.i1, 1)
+    V.tensor_copy(T.cg[:, 4 * r:4 * r + 1], T.cnb[:, r:r + 1]).then_inc(sem.cown, 1)
     V.wait_ge(sem.i1, 1)
-    V.wait_ge(sem.zf, 1)
-    V.wait_ge(sem.p0, 1)
-    V.tensor_tensor_scan(T.sc[:], T.inc[:], T.zf[:], T.p0[:, 0:1], add, mx).then_inc(sem.sc, 1)
+    V.tensor_tensor_scan(T.sc[:], T.inc[:], T.zt[:, 0:64], T.p0[:, 0:1], add, mx).then_inc(sem.sc, 1)
+
+    picks = [0, 0, 0]
+
+    def quantise_x(k):
+        a, b = X_CUTS[k], X_CUTS[k + 1]
+        V.wait_ge(sem["x%d" % k], 16)
+        V.quantize_mx(T.q[:, a:b], T.qs[:, a:b], T.xt[:, 4 * a:4 * b]).then_inc(sem["q%d" % k], 1)
+
+    def pick(k, a, b, w):
+        picks[k] += 1
+        V.tensor_copy(T.slot[:, 128 * a:128 * b].bitcast(dt.uint32),
+                      T.q[:, 0:w].bitcast(dt.uint32).indirect(T.so[:, 8 * a:8 * b])).then_inc(sem["pc%d" % k], 1)
+        A.activation(T.slots[:, 128 * a:128 * b], T.qs[:, 0:w].indirect(T.so[:, 8 * a:8 * b]),
+                     copy).then_inc(sem["pl%d" % k], 1)
+
+    quantise_x(0)
     V.wait_ge(sem.sc, 1)
     V.tensor_scalar(T.so[:], T.sc[:], float(T_COLS - 1), None, mn).then_inc(sem.so, 1)
-
-    g.wait_ge(sem.ch, 32)
-    g.remote_dma_fused([RemoteDMATransfer(dst_ids=[dst_id(d) for d in others],
-                                          dma_engine_mask=bits(topo.engines(core, cores[others[0]])[0:1]),
-                                          remote_sem=sem.cgot, srcs=[T.cin[r]], dsts=[T.cin[r] for d in others])],
-                       local_sem=sem.sent)
-    sent[0] += 1
-    Y.wait_ge(sem.ch, 32)
-    Y.wait_ge(sem.cgot, len(others))
-    Y.dma_start(T.cg[0:1, 0:16], T.cin[:, r:r + 2, 0]).then_inc(sem.cg, 16)
-
-    V.wait_ge(sem.x0, 16)
-    V.quantize_mx(T.q[:, 0:128], T.qs[:, 0:128], T.xt[:, 0:512]).then_inc(sem.q0, 1)
-    V.quantize_mx(T.q[:, 128:256], T.qs[:, 128:256], T.xt[:, 512:1024]).then_inc(sem.q1, 1)
-    V.wait_ge(sem.so, 1)
-    V.wait_ge(sem.q0, 1)
-    V.wait_ge(sem.q1, 1)
-    A.wait_ge(sem.so, 1)
-    A.wait_ge(sem.q0, 1)
-    A.wait_ge(sem.q1, 1)
+    for k, b in enumerate(X_CUTS[1:]):
+        if k + 2 < len(X_CUTS):
+            quantise_x(k + 1)
+        for q in (V, A):
+            if k == 0:
+                q.wait_ge(sem.so, 1)
+            q.wait_ge(sem["q%d" % k], 1)
+        d = b // CAPP - 1
+        if d in groups[0]:
+            pick(0, d, d + 1, b)
+    for k in (1, 2):
+        for a, b in runs(groups[k]):
+            pick(k, a, b, T_COLS)
 
     me = slice(128 * r, 128 * r + 128)
-    picks = []
-    for k, group in enumerate(groups):
-        if k == 1:
-            V.wait_ge(sem.bi, 1)
-            V.tensor_scalar(T.base[:], T.bi[:], T.p0[:, 0:1], 16.0, add, add).then_inc(sem.base, 1)
-            V.tensor_scalar(T.t9[:, 0:32 * G:G], T.bi[:], T.p0[:, 0:1], 16.0, add, add).then_inc(sem.t0, 1)
-            V.wait_ge(sem.x1, 16)
-            V.quantize_mx(T.q[:, 256:512], T.qs[:, 256:512], T.xt[:, 1024:2048]).then_inc(sem.q2, 1)
-            V.wait_ge(sem.q2, 1)
-            A.wait_ge(sem.q2, 1)
-        w = 256 if k == 0 else T_COLS
-        rr = runs([d for d in group if d != 0])
-        picks.append(len(rr))
-        for a, b in rr:
-            V.tensor_copy(T.slot[:, 128 * a:128 * b].bitcast(dt.uint32),
-                          T.q[:, 0:w].bitcast(dt.uint32).indirect(T.so[:, 8 * a:8 * b])).then_inc(sem["pc%d" % k], 1)
-            A.activation(T.slots[:, 128 * a:128 * b], T.qs[:, 0:w].indirect(T.so[:, 8 * a:8 * b]),
-                         copy).then_inc(sem["pl%d" % k], 1)
-        if 0 in group:
-            g.wait_ge(sem.q0, 1)
-        if rr:
-            g.wait_ge(sem["pc%d" % k], len(rr))
-        e = engines_for(topo, cores, r, group, False)
-        send([(d, e[d], (T.slot if d else T.q)[:, 128 * d:128 * d + 128].bitcast(dt.uint8),
-               T.land[:, me].bitcast(dt.uint8)) for d in group], sem.arrc)
-        if k == len(groups) - 1:
-            g.wait_ge(sem.cg, 16)
-            g.partition_broadcast(T.cgb[:], T.cg[0:1, 0:16], 128).then_inc(sem.cgb, 1)
-        for ks in SCALE_CALLS:
-            if ks[-1] == k:
-                for j in ks:
-                    if picks[j]:
-                        g.wait_ge(sem["pl%d" % j], picks[j])
-                both = [d for j in ks for d in groups[j]]
-                e = engines_for(topo, cores, r, both, True)
-                send([(d, e[d], (T.slots if d else T.qs)[:, 128 * d:128 * d + 128], T.lands[:, me]) for d in both],
-                     sem.arrs)
+    g.wait_ge(sem.q0, 1)
+    for scales, ks, e in calls_of(topo, cores, r):
+        for k in ks:
+            g.wait_ge(sem[("pl%d" if scales else "pc%d") % k], picks[k])
+        if scales:
+            send([(d, e[d], (T.slots if d else T.qs)[:, 128 * d:128 * d + 128], T.lands[:, me]) for d in e], sem.arrs)
+        else:
+            send([(d, e[d], (T.slot if d else T.q)[:, 128 * d:128 * d + 128].bitcast(dt.uint8),
+                   T.land[:, me].bitcast(dt.uint8)) for d in e], sem.arrc)
+    g.sem_inc(sem.wgo, 1)
+    Y.wait_ge(sem.wgo, 1)
+    for k in range(1, len(W_CUTS) - 1):
+        load_w(k)
 
-    V.tensor_copy(T.land[:, me].bitcast(dt.uint32),
-                  T.q[:].bitcast(dt.uint32).indirect(T.so[:, 8 * r:8 * r + 8])).then_inc(sem.ownc, 1)
     A.activation(T.lands[:, me], T.qs[:].indirect(T.so[:, 8 * r:8 * r + 8]), copy).then_inc(sem.owns, 1)
-    V.wait_ge(sem.k1, 1)
-    V.memset(T.keep[:, 0:32 * G:G], 0.0).then_inc(sem.k0, 1)
-    V.wait_ge(sem.zt, 1)
-    V.quantize_mx(T.land[:, ZERO:ZERO + 128], T.lands[:, ZERO:ZERO + 128], T.zt[:]).then_inc(sem.zq, 1)
-    V.wait_ge(sem.w, 16)
-    V.quantize_mx(T.wq[:], T.wqs[:], T.wt[:]).then_inc(sem.wq, 1)
 
-    V.wait_ge(sem.cgb, 1)
-    V.tensor_copy(T.cf[:], T.cgb[:, 0:16:2]).then_inc(sem.cf, 1)
-    V.tensor_scalar(T.mf[:], T.cgb[:, 0:16:2], -1.0, float(CAPP), mul, add).then_inc(sem.mf, 1)
+    V.wait_ge(sem.cown, 1)
+    V.wait_ge(sem.cgot, sum(len(count_engines(topo, cores, s)[r]) for s in others))
+    V.tensor_copy(T.cf[:], T.cg[:, 0:4 * N:4]).then_inc(sem.cf, 1)
+    V.tensor_scalar(T.mf[:], T.cg[:, 0:4 * N:4], -1.0, float(CAPP), mul, add).then_inc(sem.mf, 1)
     V.wait_ge(sem.cf, 1)
     V.tensor_tensor_scan(T.lb[:, 1:9], T.cf[:], T.cf[:], 0.0, add, mx).then_inc(sem.lb, 1)
-    V.wait_ge(sem.base, 1)
+    quantise_w(0)
+    V.wait_ge(sem.t0, 1)
     V.wait_ge(sem.mf, 1)
     V.wait_ge(sem.lb, 1)
     for s in range(N):
-        V.tensor_scalar(T.t9[:, s + 1:32 * G:G], T.base[:], T.lb[:, s + 1:s + 2], T.mf[:, s:s + 1],
+        V.tensor_scalar(T.t9[:, s + 1:32 * G:G], T.t9[:, 0:32 * G:G], T.lb[:, s + 1:s + 2], T.mf[:, s:s + 1],
                         AluOpType.is_ge, mul).then_inc(sem.t9, 1)
     V.wait_ge(sem.k0, 1)
-    V.wait_ge(sem.t0, 1)
     V.wait_ge(sem.t9, N)
     V.tensor_tensor_scan(T.s9[:], T.keep[:], T.t9[:], 0.0, mul, add).then_inc(sem.s9, 1)
     V.wait_ge(sem.s9, 1)
     V.tensor_scalar(T.ro[:], T.s9[:, N:32 * G:G], float(ZERO), None, mn).then_inc(sem.ro, 1)
+    V.tensor_copy(T.land[:, me].bitcast(dt.uint32),
+                  T.q[:].bitcast(dt.uint32).indirect(T.so[:, 8 * r:8 * r + 8])).then_inc(sem.ownc, 1)
     Y.wait_ge(sem.lb0, 1)
     Y.wait_ge(sem.lb, 1)
     Y.dma_start(T.ln[:], T.lb[0:1, 0:9]).then_inc(sem.lnst, 16)
 
     nc = ns = 0
     for s in others:
-        gs = groups_of(topo, cores, s)
-        for group in gs:
-            if r in group:
-                nc += len(engines_for(topo, cores, s, group, False)[r])
-        for ks in SCALE_CALLS:
-            both = [d for j in ks for d in gs[j]]
-            if r in both:
-                ns += len(engines_for(topo, cores, s, both, True)[r])
+        for scales, ks, e in calls_of(topo, cores, s):
+            if scales:
+                ns += len(e.get(r, []))
+            else:
+                nc += len(e.get(r, []))
     for q in (V, A):
         q.wait_ge(sem.ro, 1)
         q.wait_ge(sem.zq, 1)
@@ -270,8 +269,9 @@ def rank_program(g, core, T, topo):
                       T.land[:].bitcast(dt.uint32).indirect(T.ro[:, a // 16:b // 16])).then_inc(sem["ac%d" % i], 1)
         A.activation(T.pks[:, a:b], T.lands[:].indirect(T.ro[:, a // 16:b // 16]), copy).then_inc(sem["as%d" % i], 1)
 
-    P.wait_ge(sem.wq, 1)
     for o in range(O):
+        if o in W_CUTS[:-1]:
+            P.wait_ge(sem["wq%d" % W_CUTS.index(o)], 1)
         for i, (a, b) in enumerate(parts):
             if o == 0:
                 P.wait_ge(sem["ac%d" % i], 1)
@@ -280,22 +280,29 @@ def rank_program(g, core, T, topo):
             P.matmul_mx(T.ps[:, 512 * k:512 * k + b - a], T.wq[:, 128 * o:128 * o + 128],
                         T.wqs[:, 128 * o:128 * o + 128], T.pk[:, a:b], T.pks[:, a:b], True,
                         True).then_inc(sem["m%d" % k], 1)
-    stores = 0
-    for o in range(O):
-        at = S_COLS * o
-        V.wait_ge(sem["m%d" % (2 * o)], 1)
-        V.tensor_copy(T.yo[:, at:at + PART], T.ps[:, 1024 * o:1024 * o + PART]).then_inc(sem["yv%d" % o], 1)
-        A.wait_ge(sem["m%d" % (2 * o + 1)], 1)
-        A.activation(T.yo[:, at + PART:at + S_COLS], T.ps[:, 1024 * o + 512:1024 * o + 512 + S_COLS - PART],
-                     copy).then_inc(sem["ys%d" % o], 1)
-        cuts = [0, PART, S_COLS] if o == 0 else [0, S_COLS]
-        Y.wait_ge(sem["yv%d" % o], 1)
-        for a, b in zip(cuts, cuts[1:]):
-            if b == S_COLS:
-                Y.wait_ge(sem["ys%d" % o], 1)
-            Y.dma_start(T.y[:, at + a:at + b], T.yo[:, at + a:at + b]).then_inc(sem.yst, 16)
-            stores += 1
+
+    def copy_out(q, k):
+        o, (a, b) = k // 2, parts[k % 2]
+        q.wait_ge(sem["m%d" % k], 1)
+        out, src = T.yo[:, S_COLS * o + a:S_COLS * o + b], T.ps[:, 512 * k:512 * k + b - a]
+        (V.tensor_copy(out, src) if q is V else A.activation(out, src, copy)).then_inc(sem["y%d" % k], 1)
+
+    quantise_w(1)
+    copy_out(V, 1)
+    quantise_w(2)
+    for k in (4, 6):
+        copy_out(V, k)
+    for k in (0, 2, 3, 5, 7):
+        copy_out(A, k)
+
+    stores = [[0], [1], [2, 3], [4, 5], [6, 7]]
+    for ks in stores:
+        for k in ks:
+            Y.wait_ge(sem["y%d" % k], 1)
+        a = S_COLS * (ks[0] // 2) + parts[ks[0] % 2][0]
+        b = S_COLS * (ks[-1] // 2) + parts[ks[-1] % 2][1]
+        Y.dma_start(T.y[:, a:b], T.yo[:, a:b]).then_inc(sem.yst, 16)
 
     Y.wait_ge(sem.lnst, 16)
-    Y.wait_ge(sem.yst, 16 * stores)
+    Y.wait_ge(sem.yst, 16 * len(stores))
     g.wait_ge(sem.sent, sent[0])

@@ -3,12 +3,16 @@ from concourse.mybir import dt, AluOpType, ActivationFunctionType
 
 N, T_COLS, CAPP, S_COLS, O = 8, 512, 128, 512, 4
 ZERO = N * CAPP
-PART = 256
 G = N + 1
 X_CUTS = [0, 256, 384, 512]
 EARLY = 3
-W_CUTS = [0, 1, 2, 4]
-BIG = 4096
+W_CUTS = [0, 2, 4]
+WQ_CUTS = [0, 1, 2, 4]
+PARTS = [(384, 512), (256, 384), (0, 256)]
+BANKS = 8
+PIECES = [(0, 384, 512, "A"), (0, 256, 384, "A"), (1, 256, 512, "A"), (0, 0, 256, "A"), (1, 0, 256, "V"),
+          (2, 0, 256, "A"), (2, 256, 512, "V"), (3, 0, 256, "A"), (3, 256, 512, "V")]
+STORES = [[0], [1], [2], [3], [4], [5, 6], [7, 8]]
 
 SCRATCH = {
     "xt": ("sbuf", [128, 4 * T_COLS], "bfloat16"),
@@ -44,14 +48,15 @@ SCRATCH = {
     "s9": ("sbuf", [128, 32 * G], "float16"),
     "ro": ("sbuf", [128, 32], "uint16"),
 }
-SEMAPHORES = (["cn", "cgot", "arrc", "arrs", "sent", "pi", "bi", "zt", "zq", "incm", "cown", "wgo",
+SEMAPHORES = (["arrc%d" % i for i in range(3)] + ["arrs%d" % i for i in range(3)] + ["ro%d" % i for i in range(3)]
+              + ["cn", "cgot", "sent", "pi", "bi", "zt", "zq", "incm", "cown", "wgo",
                "lb0", "pm", "p0", "bc", "i1", "sc", "so", "ownc", "owns",
-               "cf", "mf", "lb", "k1", "k0", "t0", "t9", "s9", "ro", "lnst", "yst"]
+               "cf", "mf", "lb", "k1", "k0", "t0", "t9", "s9", "lnst", "yst"]
               + ["x%d" % i for i in range(3)] + ["q%d" % i for i in range(3)]
               + ["w%d" % i for i in range(3)] + ["wq%d" % i for i in range(3)]
               + ["pc%d" % i for i in range(3)] + ["pl%d" % i for i in range(3)]
-              + ["ac%d" % i for i in range(2)] + ["as%d" % i for i in range(2)]
-              + ["m%d" % i for i in range(2 * O)] + ["y%d" % i for i in range(2 * O)])
+              + ["ac%d" % i for i in range(4)] + ["as%d" % i for i in range(4)]
+              + ["m%d" % i for i in range(len(PIECES))] + ["y%d" % i for i in range(len(PIECES))])
 
 
 def groups_of(topo, cores, r):
@@ -59,8 +64,8 @@ def groups_of(topo, cores, r):
     rest = [d for d in range(EARLY, N) if d != r]
     near = [d for d in rest if topo.die(cores[d]) == topo.die(cores[r])]
     far = [d for d in rest if d not in near]
-    if len(far) > 2 and r % 2:
-        far = far[2:] + far[:2]
+    if r < EARLY:
+        return [early, far[2:], near + far[:2]]
     late = far + near
     return [early, late[:2], late[2:]]
 
@@ -94,6 +99,10 @@ def calls_of(topo, cores, r):
     gs = groups_of(topo, cores, r)
     order = [(False, [0]), (True, [0]), (False, [1]), (True, [1, 2]), (False, [2])]
     return [(sc, ks, engines_for(topo, cores, r, [d for k in ks for d in gs[k]], sc)) for sc, ks in order]
+
+
+def part_of(s):
+    return min(i for i, (a, b) in enumerate(PARTS) if a < CAPP * (s + 1))
 
 
 def bits(es):
@@ -136,8 +145,9 @@ def rank_program(g, core, T, topo):
         Y.dma_start(T.wt[:, a:b], T.w[:, a:b]).then_inc(sem["w%d" % k], 16)
 
     def quantise_w(k):
-        a, b = W_CUTS[k], W_CUTS[k + 1]
-        V.wait_ge(sem["w%d" % k], 16)
+        a, b = WQ_CUTS[k], WQ_CUTS[k + 1]
+        if a in W_CUTS:
+            V.wait_ge(sem["w%d" % W_CUTS.index(a)], 16)
         V.quantize_mx(T.wq[:, 128 * a:128 * b], T.wqs[:, 128 * a:128 * b],
                       T.wt[:, 512 * a:512 * b]).then_inc(sem["wq%d" % k], 1)
 
@@ -202,10 +212,10 @@ def rank_program(g, core, T, topo):
                 q.wait_ge(sem.so, 1)
             q.wait_ge(sem["q%d" % k], 1)
         d = b // CAPP - 1
-        if d in groups[0]:
-            pick(0, d, d + 1, b)
+        if d < EARLY and d != r:
+            pick(0 if d in groups[0] else 1, d, d + 1, b)
     for k in (1, 2):
-        for a, b in runs(groups[k]):
+        for a, b in runs([d for d in groups[k] if d >= EARLY]):
             pick(k, a, b, T_COLS)
 
     me = slice(128 * r, 128 * r + 128)
@@ -214,10 +224,11 @@ def rank_program(g, core, T, topo):
         for k in ks:
             g.wait_ge(sem[("pl%d" if scales else "pc%d") % k], picks[k])
         if scales:
-            send([(d, e[d], (T.slots if d else T.qs)[:, 128 * d:128 * d + 128], T.lands[:, me]) for d in e], sem.arrs)
+            send([(d, e[d], (T.slots if d else T.qs)[:, 128 * d:128 * d + 128], T.lands[:, me]) for d in e],
+                 sem["arrs%d" % part_of(r)])
         else:
             send([(d, e[d], (T.slot if d else T.q)[:, 128 * d:128 * d + 128].bitcast(dt.uint8),
-                   T.land[:, me].bitcast(dt.uint8)) for d in e], sem.arrc)
+                   T.land[:, me].bitcast(dt.uint8)) for d in e], sem["arrc%d" % part_of(r)])
     g.sem_inc(sem.wgo, 1)
     Y.wait_ge(sem.wgo, 1)
     for k in range(1, len(W_CUTS) - 1):
@@ -238,71 +249,64 @@ def rank_program(g, core, T, topo):
     for s in range(N):
         V.tensor_scalar(T.t9[:, s + 1:32 * G:G], T.t9[:, 0:32 * G:G], T.lb[:, s + 1:s + 2], T.mf[:, s:s + 1],
                         AluOpType.is_ge, mul).then_inc(sem.t9, 1)
+    quantise_w(1)
     V.wait_ge(sem.k0, 1)
     V.wait_ge(sem.t9, N)
     V.tensor_tensor_scan(T.s9[:], T.keep[:], T.t9[:], 0.0, mul, add).then_inc(sem.s9, 1)
     V.wait_ge(sem.s9, 1)
-    V.tensor_scalar(T.ro[:], T.s9[:, N:32 * G:G], float(ZERO), None, mn).then_inc(sem.ro, 1)
+    for i, (a, b) in enumerate(PARTS):
+        V.tensor_scalar(T.ro[:, a // 16:b // 16], T.s9[:, G * (a // 16) + N:G * (b // 16):G], float(ZERO), float(a), mn,
+                        AluOpType.subtract).then_inc(sem["ro%d" % i], 1)
     V.tensor_copy(T.land[:, me].bitcast(dt.uint32),
                   T.q[:].bitcast(dt.uint32).indirect(T.so[:, 8 * r:8 * r + 8])).then_inc(sem.ownc, 1)
     Y.wait_ge(sem.lb0, 1)
     Y.wait_ge(sem.lb, 1)
     Y.dma_start(T.ln[:], T.lb[0:1, 0:9]).then_inc(sem.lnst, 16)
 
-    nc = ns = 0
+    nc, ns = [0] * len(PARTS), [0] * len(PARTS)
     for s in others:
         for scales, ks, e in calls_of(topo, cores, s):
-            if scales:
-                ns += len(e.get(r, []))
-            else:
-                nc += len(e.get(r, []))
+            (ns if scales else nc)[part_of(s)] += len(e.get(r, []))
     for q in (V, A):
-        q.wait_ge(sem.ro, 1)
         q.wait_ge(sem.zq, 1)
     V.wait_ge(sem.ownc, 1)
     A.wait_ge(sem.owns, 1)
-    V.wait_ge(sem.arrc, nc)
-    A.wait_ge(sem.arrs, ns)
-    parts = [(0, PART), (PART, S_COLS)]
-    for i, (a, b) in enumerate(parts):
+    for i, (a, b) in enumerate(PARTS):
+        for q, name, n in ((V, "arrc%d", nc[i]), (A, "arrs%d", ns[i])):
+            q.wait_ge(sem["ro%d" % i], 1)
+            if n:
+                q.wait_ge(sem[name % i], n)
+        at = T.ro[:, a // 16:b // 16]
         V.tensor_copy(T.pk[:, a:b].bitcast(dt.uint32),
-                      T.land[:].bitcast(dt.uint32).indirect(T.ro[:, a // 16:b // 16])).then_inc(sem["ac%d" % i], 1)
-        A.activation(T.pks[:, a:b], T.lands[:].indirect(T.ro[:, a // 16:b // 16]), copy).then_inc(sem["as%d" % i], 1)
+                      T.land[:, a:ZERO + 128].bitcast(dt.uint32).indirect(at)).then_inc(sem["ac%d" % i], 1)
+        A.activation(T.pks[:, a:b], T.lands[:, a:ZERO + 128].indirect(at), copy).then_inc(sem["as%d" % i], 1)
 
-    for o in range(O):
-        if o in W_CUTS[:-1]:
-            P.wait_ge(sem["wq%d" % W_CUTS.index(o)], 1)
-        for i, (a, b) in enumerate(parts):
-            if o == 0:
-                P.wait_ge(sem["ac%d" % i], 1)
-                P.wait_ge(sem["as%d" % i], 1)
-            k = 2 * o + i
-            P.matmul_mx(T.ps[:, 512 * k:512 * k + b - a], T.wq[:, 128 * o:128 * o + 128],
-                        T.wqs[:, 128 * o:128 * o + 128], T.pk[:, a:b], T.pks[:, a:b], True,
-                        True).then_inc(sem["m%d" % k], 1)
-
-    def copy_out(q, k):
-        o, (a, b) = k // 2, parts[k % 2]
+    quantise_w(2)
+    waited = set()
+    for k, (o, a, b, by) in enumerate(PIECES):
+        bank = 512 * (k % BANKS)
+        need = ["wq%d" % max(i for i, c in enumerate(WQ_CUTS) if c <= o)]
+        need += [n % i for i, (c, d) in enumerate(PARTS) if c < b and a < d for n in ("ac%d", "as%d")]
+        for n in need:
+            if n not in waited:
+                waited.add(n)
+                P.wait_ge(sem[n], 1)
+        if k >= BANKS:
+            P.wait_ge(sem["y%d" % (k - BANKS)], 1)
+        P.matmul_mx(T.ps[:, bank:bank + b - a], T.wq[:, 128 * o:128 * o + 128], T.wqs[:, 128 * o:128 * o + 128],
+                    T.pk[:, a:b], T.pks[:, a:b], True, True).then_inc(sem["m%d" % k], 1)
+        out, src = T.yo[:, S_COLS * o + a:S_COLS * o + b], T.ps[:, bank:bank + b - a]
+        q = V if by == "V" else A
         q.wait_ge(sem["m%d" % k], 1)
-        out, src = T.yo[:, S_COLS * o + a:S_COLS * o + b], T.ps[:, 512 * k:512 * k + b - a]
         (V.tensor_copy(out, src) if q is V else A.activation(out, src, copy)).then_inc(sem["y%d" % k], 1)
 
-    quantise_w(1)
-    copy_out(V, 1)
-    quantise_w(2)
-    for k in (4, 6):
-        copy_out(V, k)
-    for k in (0, 2, 3, 5, 7):
-        copy_out(A, k)
-
-    stores = [[0], [1], [2, 3], [4, 5], [6, 7]]
-    for ks in stores:
+    for ks in STORES:
         for k in ks:
             Y.wait_ge(sem["y%d" % k], 1)
-        a = S_COLS * (ks[0] // 2) + parts[ks[0] % 2][0]
-        b = S_COLS * (ks[-1] // 2) + parts[ks[-1] % 2][1]
+        a = S_COLS * PIECES[ks[0]][0] + PIECES[ks[0]][1]
+        b = S_COLS * PIECES[ks[-1]][0] + PIECES[ks[-1]][2]
         Y.dma_start(T.y[:, a:b], T.yo[:, a:b]).then_inc(sem.yst, 16)
 
     Y.wait_ge(sem.lnst, 16)
-    Y.wait_ge(sem.yst, 16 * len(stores))
+    Y.wait_ge(sem.yst, 16 * len(STORES))
     g.wait_ge(sem.sent, sent[0])

@@ -2,17 +2,46 @@ from concourse.bass import DstId, RemoteDMATransfer
 from concourse.mybir import dt, AluOpType, ActivationFunctionType
 
 N, T_COLS, CAPP, S_COLS, O = 8, 512, 128, 512, 4
-ZERO = N * CAPP
-G = N + 1
-X_CUTS = [0, 256, 384, 512]
+GMAX = N + 1
+WIN = (N + 1) * CAPP
+FAR = 4096.0
+X_CUTS = [0, 128, 256, 384, 512]
 EARLY = 3
-W_CUTS = [0, 2, 4]
-WQ_CUTS = [0, 1, 2, 4]
-PARTS = [(384, 512), (256, 384), (0, 256)]
+W_LOADS = [[0, 1], [2], [3]]
+GROUPS = ["ffn", "fn", "fn"]
+SWAP = True
+BETWEEN = [1]
+S0_TWO = False
+S0_PAD = False
+JOIN0 = False
+W_AHEAD = 1
+DEAL = {}
+ALLB, LAG, WPRE = False, 0, False
+AHEAD = []
+ORDER = ["s0", "c0", "c1", "s1", "c2"]
+TURN = -1
+SHIFT = 0
+CALM = 0
+CALM_GROUPS, CALM_ORDER = ["ffff", "nnn"], ["c0", "s1", "c1"]
+SEGMENTS = [[0, 1], [2], [3, 4], [5, 6], [7]]
+SEGMENTS0 = [[0], [1], [2], [3], [4], [5], [6], [7]]
+OWN_DMA = True
+OWN0_DMA = True
+GROUPS0 = ["ffn", "fn", "fn"]
+FIRST, FIRST_FROM = False, 3
+FIRST_ORDER = ["c0", "s0", "c1", "s1", "c2"]
+HEAD = "q0 s q1 l"
+X_BY_A = [0]
+MID = {}
+PARTS = [(384, 512), (192, 384), (0, 192)]
+HALVES = [(256, 512), (0, 256)]
 BANKS = 8
-PIECES = [(0, 384, 512, "A"), (0, 256, 384, "A"), (1, 256, 512, "A"), (0, 0, 256, "A"), (1, 0, 256, "V"),
-          (2, 0, 256, "A"), (2, 256, 512, "V"), (3, 0, 256, "A"), (3, 256, 512, "V")]
-STORES = [[0], [1], [2], [3], [4], [5, 6], [7, 8]]
+PIECES = [(0, 384, 512), (1, 384, 512), (0, 192, 384), (1, 192, 384), (0, 0, 192), (1, 0, 192),
+          (2, 0, 288), (2, 288, 512), (3, 0, 320), (3, 320, 512)]
+STORES = [[0], [1], [2], [3], [4], [5], [6, 7], [8, 9]]
+TAIL_V = "o0 l0 t0 h0 h1 r0 r1 w0 w1 c0 c1 c2 w2 w3 y4 y5 y7 y9"
+TAIL_V0 = "o0 l0 t0 h0 h1 r0 r1 w0 w1 c0 c1 c2 w2 w3 y4 y5 y7 y9"
+TAIL_A = "o0 s0 s1 s2 y0 y1 y2 y3 y6 y8"
 
 SCRATCH = {
     "xt": ("sbuf", [128, 4 * T_COLS], "bfloat16"),
@@ -22,16 +51,16 @@ SCRATCH = {
     "qs": ("sbuf", [128, T_COLS], "uint8"),
     "slot": ("sbuf", [128, N * CAPP], "float8_e4m3fn_x4"),
     "slots": ("sbuf", [128, N * CAPP], "uint8"),
-    "land": ("sbuf", [128, ZERO + 128], "float8_e4m3fn_x4"),
-    "lands": ("sbuf", [128, ZERO + 128], "uint8"),
+    "land": ("sbuf", [128, WIN], "float8_e4m3fn_x4"),
+    "lands": ("sbuf", [128, WIN], "uint8"),
     "wq": ("sbuf", [128, 128 * O], "float8_e4m3fn_x4"),
     "wqs": ("sbuf", [128, 128 * O], "uint8"),
-    "pk": ("sbuf", [128, S_COLS], "float8_e4m3fn_x4"),
-    "pks": ("sbuf", [128, S_COLS], "uint8"),
+    "pk": ("sbuf", [128, S_COLS + 128], "float8_e4m3fn_x4"),
+    "pks": ("sbuf", [128, S_COLS + 128], "uint8"),
     "yo": ("sbuf", [128, O * S_COLS], "float32"),
-    "ps": ("psum", [128, 512 * 2 * O], "float32"),
+    "ps": ("psum", [128, 512 * BANKS], "float32"),
     "cn1": ("sbuf", [128, 16], "int32"),
-    "cnb": ("sbuf", [128, 8], "int32"),
+    "cnb": ("sbuf", [128, 72], "int32"),
     "pi": ("sbuf", [128, 8], "int32"),
     "pm": ("sbuf", [128, 8], "int32"),
     "p0": ("sbuf", [128, 8], "float32"),
@@ -40,69 +69,104 @@ SCRATCH = {
     "sc": ("sbuf", [128, 64], "float32"),
     "so": ("sbuf", [128, 64], "uint16"),
     "cg": ("sbuf", [128, 4 * N], "int32"),
-    "cf": ("sbuf", [128, 8], "float32"),
+    "back": ("sbuf", [128, 8], "float32"),
     "mf": ("sbuf", [128, 8], "float32"),
     "lb": ("sbuf", [128, 16], "float32"),
-    "keep": ("sbuf", [128, 32 * G], "bfloat16"),
-    "t9": ("sbuf", [128, 32 * G], "float16"),
-    "s9": ("sbuf", [128, 32 * G], "float16"),
+    "ar": ("sbuf", [128, 32], "float16"),
+    "keep": ("sbuf", [128, 32 * GMAX], "float16"),
+    "t9": ("sbuf", [128, 32 * GMAX], "float16"),
+    "s9": ("sbuf", [128, 32 * GMAX], "float16"),
     "ro": ("sbuf", [128, 32], "uint16"),
 }
-SEMAPHORES = (["arrc%d" % i for i in range(3)] + ["arrs%d" % i for i in range(3)] + ["ro%d" % i for i in range(3)]
-              + ["cn", "cgot", "sent", "pi", "bi", "zt", "zq", "incm", "cown", "wgo",
-               "lb0", "pm", "p0", "bc", "i1", "sc", "so", "ownc", "owns",
-               "cf", "mf", "lb", "k1", "k0", "t0", "t9", "s9", "lnst", "yst"]
-              + ["x%d" % i for i in range(3)] + ["q%d" % i for i in range(3)]
-              + ["w%d" % i for i in range(3)] + ["wq%d" % i for i in range(3)]
-              + ["pc%d" % i for i in range(3)] + ["pl%d" % i for i in range(3)]
-              + ["ac%d" % i for i in range(4)] + ["as%d" % i for i in range(4)]
-              + ["m%d" % i for i in range(len(PIECES))] + ["y%d" % i for i in range(len(PIECES))])
+SEMAPHORES = (["cn", "cgot", "sent", "pi", "bi", "zt", "zq", "zp", "incm", "cown", "wgo", "lb0", "pm", "p0", "bc", "i1", "cz",
+               "sc", "so", "oc", "os_", "mf", "lb", "k1", "k0", "k2", "back", "ar", "t0", "t9", "lnst", "yst"]
+              + [n % i for n in ("arrc%d", "arrs%d", "h%d", "r%d", "x%d", "q%d", "w%d", "wq%d", "pc%d", "ps%d", "ac%d",
+                                 "as%d") for i in range(5)]
+              + ["m%d" % i for i in range(16)] + ["y%d" % i for i in range(16)])
 
 
 def groups_of(topo, cores, r):
-    early = [d for d in range(EARLY) if d != r]
-    rest = [d for d in range(EARLY, N) if d != r]
-    near = [d for d in rest if topo.die(cores[d]) == topo.die(cores[r])]
-    far = [d for d in rest if d not in near]
-    if r < EARLY:
-        return [early, far[2:], near + far[:2]]
-    late = far + near
-    return [early, late[:2], late[2:]]
+    mine = [d for d in range(N) if topo.die(cores[d]) == topo.die(cores[r])]
+    far = [d for d in range(N) if d not in mine]
+    i = mine.index(r)
+    left = {"f": [far[(TURN * i + k + SHIFT) % len(far)] for k in range(len(far))],
+            "n": [mine[(i + k) % len(mine)] for k in range(1, len(mine))]}
+    if SWAP:
+        if 0 in far:
+            far = far[:1] + far[-1:] + far[1:-1]
+        left["f"] = [far[k ^ i ^ SHIFT] for k in range(len(far))]
+    if FIRST and r >= FIRST_FROM:
+        late = [d for d in left["f"] + left["n"] if d >= EARLY]
+        early = [d for d in range(EARLY) if d != r]
+        return [early, late[:len(late) - 2], late[-2:]]
+    if AHEAD:
+        far, near = ([d for d in left[c] if d not in AHEAD] for c in "fn")
+        pairs = [[far.pop(), near.pop()] for k in range(2)]
+        return [[d for d in AHEAD if d != r], far + near] + pairs[::-1]
+    return [[left[c].pop(0) for c in grp] for grp in (GROUPS if r else GROUPS0)]
 
 
-def engines_for(topo, cores, r, group, scales):
-    e = topo.engines(cores[r], cores[group[0]])
-    fars = [d for d in group if topo.die(cores[d]) != topo.die(cores[r])]
-    nears = [d for d in group if d not in fars]
-    a, b = (e[1::2], e[0::2]) if scales else (e[0::2], e[1::2])
-    h = len(a) // 2
-    if len(group) == 2:
-        cut = [a, b]
-    elif len(group) == 3:
-        cut = [b[:h], b[h:], a] if len(fars) == 2 else [a, b[:h], b[h:]]
-    elif len(group) == 4:
-        cut = [a[:h], a[h:], b[:h], b[h:]]
-    elif len(group) == 5:
-        cut = [a[:h], a[h:], b[:h], b[h:h + h // 2], b[h + h // 2:]]
-    else:
-        cut = [a[i:i + 2] for i in range(0, len(a), 2)] + [b[0:2], b[2:4], b[4:]]
-    return {d: c for d, c in zip(fars + nears, cut)}
-
-
-def count_engines(topo, cores, r):
-    others = [d for d in range(N) if d != r]
-    e = topo.engines(cores[r], cores[others[0]])
-    return {d: (e[2 * i + 2:2 * i + 4] if i else e[0:4]) for i, d in enumerate(others)}
+def split(es, k):
+    size = [1] * k
+    while sum(size) + min(size) <= len(es):
+        size[size.index(min(size))] *= 2
+    at = [sum(size[:i]) for i in range(k + 1)]
+    return [es[x:y] for x, y in zip(at, at[1:])]
 
 
 def calls_of(topo, cores, r):
+    others = [d for d in range(N) if d != r]
+    e = topo.engines(cores[r], cores[others[0]])
     gs = groups_of(topo, cores, r)
-    order = [(False, [0]), (True, [0]), (False, [1]), (True, [1, 2]), (False, [2])]
-    return [(sc, ks, engines_for(topo, cores, r, [d for k in ks for d in gs[k]], sc)) for sc, ks in order]
+    early = EARLY if r >= CALM else 0
+    dests = {"n": others, "s0": [d for d in others if d < early], "s1": [d for d in others if d >= early]}
+    if JOIN0 and not r:
+        dests.update({"s0": others[:3], "s1": others[3:]})
+    if S0_PAD:
+        dests.update({"s0": others[:3], "s1": others[3:]})
+    dests.update({"c%d" % k: grp for k, grp in enumerate(gs)})
+    a, b = e[0::2], e[1::2]
+    out = []
+    for name in ["n"] + (FIRST_ORDER if FIRST and r >= FIRST_FROM else ORDER):
+        far = [d for d in dests[name] if topo.die(cores[d]) != topo.die(cores[r])]
+        near = [d for d in dests[name] if d not in far]
+        k = len(far + near)
+        if not k:
+            continue
+        if name[0] == "c" and far and near and k != 4:
+            cut = split(a, len(far)) + split(b, len(near))
+        elif name == "s0" and S0_TWO:
+            cut = split(b, 2)
+        elif name == "s1" and S0_TWO:
+            light, rest = split(a, 2)
+            cut = split(b, 2) + [rest] + split(light, 2)
+        elif name[0] == "s" and k % 2:
+            cut = split(b, k // 2 + 1) + split(a, k // 2)
+        else:
+            cut = split(a + b, k)
+        if name + str(k) in DEAL:
+            quarter = dict(zip("ABCD", split(a, 2) + split(b, 2)))
+            half = dict(zip("abcdefgh", split(a, 4) + split(b, 4)))
+            cut = [sum([quarter.get(x) or half[x] for x in w], []) for w in DEAL[name + str(k)].split()]
+        out.append((name, dict(zip(far + near, cut))))
+    return out
 
 
-def part_of(s):
-    return min(i for i, (a, b) in enumerate(PARTS) if a < CAPP * (s + 1))
+def segments(d):
+    return SEGMENTS if d else SEGMENTS0
+
+
+def slot_of(s, d):
+    seg = [x for x in segments(d) if s in x][0]
+    return CAPP * (N - seg[-1] + seg.index(s))
+
+
+def window(a, d):
+    return CAPP * (N + 1 - [x for x in segments(d) if a // CAPP in x][0][0])
+
+
+def part_of(s, d):
+    return min(i for i, (a, b) in enumerate(PARTS) if slot_of(s, d) < window(a, d))
 
 
 def bits(es):
@@ -128,183 +192,268 @@ def rank_program(g, core, T, topo):
     V, A, P, Y, sem = g.vector, g.scalar, g.tensor, g.sync, T.sem
     copy = ActivationFunctionType.Copy
     add, mx, mn, mul = AluOpType.add, AluOpType.max, AluOpType.min, AluOpType.mult
-    groups = groups_of(topo, cores, r)
+    calls = calls_of(topo, cores, r)
     sent = [0]
+    segs = segments(r)
+    G = len(segs) + 1
+    a0 = segs[0][-1]
+    first = 0 if [r, r + 1] in SEGMENTS else 1
+    low = 0 if [r, r + 1] in SEGMENTS0 else 1
 
-    def send(items, rsem):
+    def at(d):
+        return slice(slot_of(r, d), slot_of(r, d) + CAPP)
+
+    narrow = any(b - a < 128 for o, a, b in PIECES)
+    waited = set()
+
+    def need(q, names):
+        for n in names:
+            key = ([q is x for x in (V, A, P)].index(True), n)
+            if key not in waited:
+                waited.add(key)
+                q.wait_ge(sem[n], 1)
+
+    def send(items):
         out = []
-        for d, es, src, dst in items:
+        for d, es, src, dst, rsem in items:
             rid, pid, _ = topo.addr(cores[d])
             sent[0] += len(es)
             out.append(RemoteDMATransfer(dst_ids=[DstId(rid=rid, pnc=pid)], dma_engine_mask=bits(es), remote_sem=rsem,
                                          srcs=[src], dsts=[dst]))
         g.remote_dma_fused(out, local_sem=sem.sent)
 
-    def load_w(k):
-        a, b = 512 * W_CUTS[k], 512 * W_CUTS[k + 1]
-        Y.dma_start(T.wt[:, a:b], T.w[:, a:b]).then_inc(sem["w%d" % k], 16)
+    def load_w(tiles):
+        a, b = tiles[0], tiles[-1] + 1
+        Y.dma_start(T.wt[:, 512 * a:512 * b], T.w[:, 512 * a:512 * b]).then_inc(sem["w%d" % a], 16)
 
-    def quantise_w(k):
-        a, b = WQ_CUTS[k], WQ_CUTS[k + 1]
-        if a in W_CUTS:
-            V.wait_ge(sem["w%d" % W_CUTS.index(a)], 16)
-        V.quantize_mx(T.wq[:, 128 * a:128 * b], T.wqs[:, 128 * a:128 * b],
-                      T.wt[:, 512 * a:512 * b]).then_inc(sem["wq%d" % k], 1)
+    def move(q, out, src):
+        return V.tensor_copy(out, src) if q is V else A.activation(out, src, copy)
 
     Y.dma_start(T.cn1[0:1, 0:16], T.cn[:]).then_inc(sem.cn, 16)
     for k, (a, b) in enumerate(zip(X_CUTS, X_CUTS[1:])):
-        Y.dma_start(T.xt[:, 4 * a:4 * b], T.x[:, 4 * a:4 * b]).then_inc(sem["x%d" % k], 16)
-    load_w(0)
+        (A if k in X_BY_A else Y).dma_start(T.xt[:, 4 * a:4 * b], T.x[:, 4 * a:4 * b]).then_inc(sem["x%d" % k], 16)
+    for tiles in W_LOADS[:W_AHEAD]:
+        load_w(tiles)
 
     g.iota(T.pi[:, 0:1], [[1, 1]], 0, 1).then_inc(sem.pi, 1)
     g.iota(T.bi[:], [[16, 32]], 0, 0).then_inc(sem.bi, 1)
-    V.memset(T.zt[:], 0.0).then_inc(sem.zt, 1)
     V.memset(T.inc[:], 16.0).then_inc(sem.incm, 1)
-    V.memset(T.keep[:], 1.0).then_inc(sem.k1, 1)
+    V.memset(T.cnb[:], 0).then_inc(sem.cz, 1)
+    V.memset(T.keep[:, 0:32 * G], 0.0).then_inc(sem.k1, 1)
     V.wait_ge(sem.pi, 1)
     V.tensor_scalar(T.pm[:, 0:1], T.pi[:, 0:1], 15, None, AluOpType.bitwise_and).then_inc(sem.pm, 1)
-    V.memset(T.lb[:, 0:1], 0.0).then_inc(sem.lb0, 1)
+    V.memset(T.zt[:], 0.0).then_inc(sem.zt, 1)
     V.wait_ge(sem.pm, 1)
     V.tensor_scalar(T.p0[:, 0:1], T.pm[:, 0:1], -16.0, None, add).then_inc(sem.p0, 1)
+    V.memset(T.t9[:, G - 1:32 * G:G], FAR).then_inc(sem.t0, 1)
+
+    def fill(buf, x, z, value):
+        return A.activation(buf[:, x:z], T.inc[:, 1:1 + z - x], copy, scale=value / 16.0)
+
+    A.wait_ge(sem.incm, 1)
+    jumps = T.inc[:, 8 * first:64:8]
+    A.activation(jumps, jumps, copy, scale=1.0 - CAPP / 16.0).then_inc(sem.i1, 1)
+    fill(T.lb, 0, 1, 0.0).then_inc(sem.lb0, 1)
+    back = [0] * N
+    for x, z in zip(segs, segs[1:]):
+        back[z[-1] - 1] = slot_of(z[-1], r) - slot_of(x[-1], r)
+    cuts = [j for j in range(a0, N - 1) if j == a0 or back[j] != back[j - 1]] + [N - 1]
+    for x, z in zip(cuts, cuts[1:]):
+        fill(T.back, x, z, float(back[x])).then_inc(sem.back, 1)
     V.wait_ge(sem.k1, 1)
-    V.memset(T.keep[:, 0:32 * G:G], 0.0).then_inc(sem.k0, 1)
+    V.memset(T.keep[:, 0:32 * G:G], FAR).then_inc(sem.k0, 1)
     V.wait_ge(sem.bi, 1)
     V.wait_ge(sem.p0, 1)
-    V.tensor_scalar(T.t9[:, 0:32 * G:G], T.bi[:], T.p0[:, 0:1], 16.0, add, add).then_inc(sem.t0, 1)
+    V.tensor_scalar(T.ar[:], T.bi[:], T.p0[:, 0:1], 16.0, add, add).then_inc(sem.ar, 1)
+    V.tensor_scalar(T.keep[:, G - 1:32 * G:G], T.bi[:], T.p0[:, 0:1], 16.0, add, add).then_inc(sem.k2, 1)
     V.wait_ge(sem.zt, 1)
-    V.quantize_mx(T.land[:, ZERO:ZERO + 128], T.lands[:, ZERO:ZERO + 128], T.zt[:]).then_inc(sem.zq, 1)
+    V.quantize_mx(T.land[:, 0:CAPP], T.lands[:, 0:CAPP], T.zt[:]).then_inc(sem.zq, 1)
+    if narrow:
+        V.quantize_mx(T.pk[:, S_COLS:], T.pks[:, S_COLS:], T.zt[:]).then_inc(sem.zp, 1)
+        need(P, ["zp"])
 
+    def count(d):
+        return T.cnb[:, 8 * (first + d):8 * (first + d) + 1]
+
+    g.wait_ge(sem.cz, 1)
     g.wait_ge(sem.cn, 16)
-    g.partition_broadcast(T.cnb[:], T.cn1[0:1, 0:8], 128).then_inc(sem.bc, 1)
+    g.partition_broadcast(T.cnb[:, 8 * first:8 * (first + N):8], T.cn1[0:1, 0:N], 128).then_inc(sem.bc, 1)
     g.wait_ge(sem.bc, 1)
-    e = count_engines(topo, cores, r)
-    send([(d, e[d], T.cnb[:, d:d + 1], T.cg[:, 4 * r:4 * r + 1]) for d in others], sem.cgot)
-
-    V.wait_ge(sem.bc, 1)
-    V.wait_ge(sem.incm, 1)
-    V.tensor_scalar(T.inc[:, 8:64:8], T.cnb[:, 0:7], -112.0, None, add).then_inc(sem.i1, 1)
-    V.tensor_copy(T.cg[:, 4 * r:4 * r + 1], T.cnb[:, r:r + 1]).then_inc(sem.cown, 1)
-    V.wait_ge(sem.i1, 1)
-    V.tensor_tensor_scan(T.sc[:], T.inc[:], T.zt[:, 0:64], T.p0[:, 0:1], add, mx).then_inc(sem.sc, 1)
-
-    picks = [0, 0, 0]
+    e = calls[0][1]
+    send([(d, e[d], count(d), T.cg[:, 4 * r:4 * r + 1], sem.cgot) for d in e])
+    if OWN_DMA:
+        Y.wait_ge(sem.bc, 1)
+        Y.dma_start(T.cg[:, 4 * r:4 * r + 1], count(r)).then_inc(sem.cown, 16)
+    if OWN0_DMA and r < low:
+        Y.wait_ge(sem.q0, 1)
+        Y.dma_start(T.lands[:, at(r)], T.qs[:, 0:CAPP]).then_inc(sem.os_, 16)
+        Y.dma_start(T.land[:, at(r)].bitcast(dt.uint8), T.q[:, 0:CAPP].bitcast(dt.uint8)).then_inc(sem.oc, 16)
 
     def quantise_x(k):
         a, b = X_CUTS[k], X_CUTS[k + 1]
         V.wait_ge(sem["x%d" % k], 16)
         V.quantize_mx(T.q[:, a:b], T.qs[:, a:b], T.xt[:, 4 * a:4 * b]).then_inc(sem["q%d" % k], 1)
 
-    def pick(k, a, b, w):
-        picks[k] += 1
-        V.tensor_copy(T.slot[:, 128 * a:128 * b].bitcast(dt.uint32),
-                      T.q[:, 0:w].bitcast(dt.uint32).indirect(T.so[:, 8 * a:8 * b])).then_inc(sem["pc%d" % k], 1)
-        A.activation(T.slots[:, 128 * a:128 * b], T.qs[:, 0:w].indirect(T.so[:, 8 * a:8 * b]),
-                     copy).then_inc(sem["pl%d" % k], 1)
-
-    quantise_x(0)
-    V.wait_ge(sem.sc, 1)
-    V.tensor_scalar(T.so[:], T.sc[:], float(T_COLS - 1), None, mn).then_inc(sem.so, 1)
-    for k, b in enumerate(X_CUTS[1:]):
-        if k + 2 < len(X_CUTS):
-            quantise_x(k + 1)
-        for q in (V, A):
-            if k == 0:
-                q.wait_ge(sem.so, 1)
-            q.wait_ge(sem["q%d" % k], 1)
-        d = b // CAPP - 1
-        if d < EARLY and d != r:
-            pick(0 if d in groups[0] else 1, d, d + 1, b)
-    for k in (1, 2):
-        for a, b in runs([d for d in groups[k] if d >= EARLY]):
-            pick(k, a, b, T_COLS)
-
-    me = slice(128 * r, 128 * r + 128)
-    g.wait_ge(sem.q0, 1)
-    for scales, ks, e in calls_of(topo, cores, r):
-        for k in ks:
-            g.wait_ge(sem[("pl%d" if scales else "pc%d") % k], picks[k])
-        if scales:
-            send([(d, e[d], (T.slots if d else T.qs)[:, 128 * d:128 * d + 128], T.lands[:, me]) for d in e],
-                 sem["arrs%d" % part_of(r)])
+    for word in HEAD.split():
+        if word == "s":
+            need(V, ["bc", "i1"])
+            V.tensor_tensor_scan(T.sc[:], T.cnb[:, 0:64], T.inc[:], T.p0[:, 0:1], add, add).then_inc(sem.sc, 1)
+        elif word == "l":
+            V.wait_ge(sem.sc, 1)
+            V.tensor_scalar(T.so[:], T.sc[:], float(T_COLS - 1), None, mn).then_inc(sem.so, 1)
         else:
-            send([(d, e[d], (T.slot if d else T.q)[:, 128 * d:128 * d + 128].bitcast(dt.uint8),
-                   T.land[:, me].bitcast(dt.uint8)) for d in e], sem["arrc%d" % part_of(r)])
-    g.sem_inc(sem.wgo, 1)
+            quantise_x(int(word[1:]))
+
+    call_of = {(name[0], d): name for name, deal in calls for d in deal}
+    picks = {name: 0 for name, deal in calls}
+
+    def pick(kind, a, b, out=None, done=None):
+        w = min(T_COLS, CAPP * b)
+        q = V if kind == "c" else A
+        need(q, ["so"] + ["q%d" % k for k, c in enumerate(X_CUTS[:-1]) if c < w])
+        if done is None:
+            done = "p" + call_of[kind, a]
+            picks[call_of[kind, a]] += 1
+        if out is None:
+            out = (T.slot if kind == "c" else T.slots)[:, 128 * a:128 * b]
+        win = T.qs[:, 0:w]
+        if kind == "c":
+            out, win = out.bitcast(dt.uint32), T.q[:, 0:w].bitcast(dt.uint32)
+        move(q, out, win.indirect(T.so[:, 8 * a:8 * b])).then_inc(sem[done], 1)
+
+    landed = {(k, i): 0 for k in "cs" for i in range(len(PARTS))}
+    for s in others:
+        for name, e in calls_of(topo, cores, s)[1:]:
+            landed[name[0], part_of(s, r)] += len(e.get(r, []))
+    cg = T.cg[:, 0:4 * N:4]
+
+    def step(q, kind, i):
+        if kind == "o":
+            if r >= low:
+                pick(*(("c", r, r + 1, T.land[:, at(r)], "oc") if q is V else
+                       ("s", r, r + 1, T.lands[:, at(r)], "os_")))
+            elif q is V and not OWN0_DMA:
+                V.quantize_mx(T.land[:, at(r)], T.lands[:, at(r)], T.xt[:, 0:4 * CAPP]).then_inc(sem.oc, 1)
+        elif kind == "w":
+            if i in [tiles[0] for tiles in W_LOADS]:
+                V.wait_ge(sem["w%d" % i], 16)
+            V.quantize_mx(T.wq[:, 128 * i:128 * i + 128], T.wqs[:, 128 * i:128 * i + 128],
+                          T.wt[:, 512 * i:512 * i + 512]).then_inc(sem["wq%d" % i], 1)
+        elif kind == "n":
+            if not OWN_DMA:
+                V.tensor_copy(T.cg[:, 4 * r:4 * r + 1], count(r)).then_inc(sem.cown, 1)
+        elif kind == "l":
+            V.wait_ge(sem.cown, 16 if OWN_DMA else 1)
+            V.wait_ge(sem.cgot, sum(len(calls_of(topo, cores, s)[0][1][r]) for s in others))
+            V.tensor_tensor_scan(T.lb[:, 1:9], cg, cg, 0.0, add, mx).then_inc(sem.lb, 1)
+            V.wait_ge(sem.back, len(cuts) - 1)
+            V.tensor_tensor_scan(T.mf[:, a0:N - 1], T.back[:, a0:N - 1], T.cg[:, 4 * a0:4 * (N - 1):4], 0.0, add,
+                                 AluOpType.subtract).then_inc(sem.mf, 1)
+        elif kind == "t":
+            need(V, ["ar", "lb"])
+            V.tensor_scalar(T.t9[:, G - 2:32 * G:G], T.ar[:], T.lb[:, N:N + 1], -FAR, AluOpType.is_ge,
+                            mul).then_inc(sem.t9, 1)
+            need(V, ["mf"])
+            for k, x in enumerate(segs[1:]):
+                V.tensor_scalar(T.t9[:, k:32 * G:G], T.ar[:], T.lb[:, x[0]:x[0] + 1], T.mf[:, x[-1] - 1:x[-1]],
+                                AluOpType.is_ge, mul).then_inc(sem.t9, 1)
+        elif kind == "h":
+            if i == 0:
+                need(V, ["k0", "k2", "t0"])
+                V.wait_ge(sem.t9, G - 1)
+            h = slice(G * (HALVES[i][0] // 16), G * (HALVES[i][1] // 16))
+            V.tensor_tensor_scan(T.s9[:, h], T.keep[:, h], T.t9[:, h], 0.0, add, mn).then_inc(sem["h%d" % i], 1)
+        elif kind == "r":
+            a, b = HALVES[i][0] // 16, HALVES[i][1] // 16
+            need(V, ["h%d" % i, "lb0"])
+            V.tensor_scalar(T.ro[:, a:b], T.s9[:, G * a + G - 1:G * b:G], T.lb[:, a0:a0 + 1], float(slot_of(a0, r)),
+                            AluOpType.subtract, add).then_inc(sem["r%d" % i], 1)
+        elif kind == "y":
+            o, a, b = PIECES[i]
+            bank = 512 * (i % BANKS)
+            need(q, ["m%d" % i])
+            move(q, T.yo[:, S_COLS * o + a:S_COLS * o + b], T.ps[:, bank:bank + b - a]).then_inc(sem["y%d" % i], 1)
+        else:
+            a, b = PARTS[i]
+            need(q, ["zq"] + ["r%d" % k for k, (c, d) in enumerate(HALVES) if c < b and a < d])
+            if part_of(r, r) <= i:
+                if r < low and OWN0_DMA:
+                    q.wait_ge(sem["oc" if kind == "c" else "os_"], 16)
+                else:
+                    need(q, ["oc" if kind == "c" or r < low else "os_"])
+            if landed[kind, i]:
+                q.wait_ge(sem["arr%s%d" % (kind, i)], landed[kind, i])
+            w = window(a, r)
+            out, win = T.pks[:, a:b], T.lands[:, 0:w]
+            if kind == "c":
+                out, win = T.pk[:, a:b].bitcast(dt.uint32), T.land[:, 0:w].bitcast(dt.uint32)
+            move(q, out, win.indirect(T.ro[:, a // 16:b // 16])).then_inc(sem["a%s%d" % (kind, i)], 1)
+
+    def steps(q, words):
+        for word in words:
+            step(q, word[0], int(word[1:]))
+
+    pairs = []
+    early = EARLY if r >= CALM else 0
+    mid = MID.get(r, {})
+    for k in range(1, len(X_CUTS) - 1):
+        if "q%d" % k not in HEAD:
+            quantise_x(k)
+        allb = FIRST and r >= FIRST_FROM
+        for d in ([1, 2] if allb else BETWEEN):
+            group = dict(calls)["c0"]
+            if (d in group and 0 not in group or allb and d != r) and CAPP * (d + 1) == X_CUTS[k + LAG]:
+                pick("c", d, d + 1)
+                pairs.append((d, d + 1))
+    for name, deal in calls:
+        if name[0] == "c":
+            steps(V, mid.get(name, "").split())
+            rest = [d for d in deal if d >= low and (d, d + 1) not in pairs]
+            alone = early if r or not JOIN0 else 2
+            for a, b in [(d, d + 1) for d in rest if d < alone] + runs([d for d in rest if d >= alone]):
+                pick("c", a, b)
+                pairs.append((a, b))
+    for a, b in sorted(pairs, key=lambda p: min(p[0], EARLY + S0_PAD)):
+        pick("s", a, b)
+
+    g.wait_ge(sem.q0, 1)
+    for name, e in calls[1:]:
+        if picks[name]:
+            g.wait_ge(sem["p" + name], picks[name])
+        if WPRE and name == calls[-1][0]:
+            g.sem_inc(sem.wgo, 1)
+        if name[0] == "s":
+            send([(d, e[d], (T.slots if d >= low else T.qs)[:, 128 * d:128 * d + 128], T.lands[:, at(d)],
+                   sem["arrs%d" % part_of(r, d)]) for d in e])
+        else:
+            send([(d, e[d], (T.slot if d >= low else T.q)[:, 128 * d:128 * d + 128].bitcast(dt.uint8),
+                   T.land[:, at(d)].bitcast(dt.uint8), sem["arrc%d" % part_of(r, d)]) for d in e])
+    if not WPRE:
+        g.sem_inc(sem.wgo, 1)
     Y.wait_ge(sem.wgo, 1)
-    for k in range(1, len(W_CUTS) - 1):
-        load_w(k)
+    for tiles in W_LOADS[W_AHEAD:]:
+        load_w(tiles)
 
-    A.activation(T.lands[:, me], T.qs[:].indirect(T.so[:, 8 * r:8 * r + 8]), copy).then_inc(sem.owns, 1)
+    done = " ".join(mid.values()).split()
+    steps(V, [word for word in (TAIL_V if r else TAIL_V0).split() if word not in done])
+    steps(A, TAIL_A.split())
 
-    V.wait_ge(sem.cown, 1)
-    V.wait_ge(sem.cgot, sum(len(count_engines(topo, cores, s)[r]) for s in others))
-    V.tensor_copy(T.cf[:], T.cg[:, 0:4 * N:4]).then_inc(sem.cf, 1)
-    V.tensor_scalar(T.mf[:], T.cg[:, 0:4 * N:4], -1.0, float(CAPP), mul, add).then_inc(sem.mf, 1)
-    V.wait_ge(sem.cf, 1)
-    V.tensor_tensor_scan(T.lb[:, 1:9], T.cf[:], T.cf[:], 0.0, add, mx).then_inc(sem.lb, 1)
-    quantise_w(0)
-    V.wait_ge(sem.t0, 1)
-    V.wait_ge(sem.mf, 1)
-    V.wait_ge(sem.lb, 1)
-    for s in range(N):
-        V.tensor_scalar(T.t9[:, s + 1:32 * G:G], T.t9[:, 0:32 * G:G], T.lb[:, s + 1:s + 2], T.mf[:, s:s + 1],
-                        AluOpType.is_ge, mul).then_inc(sem.t9, 1)
-    quantise_w(1)
-    V.wait_ge(sem.k0, 1)
-    V.wait_ge(sem.t9, N)
-    V.tensor_tensor_scan(T.s9[:], T.keep[:], T.t9[:], 0.0, mul, add).then_inc(sem.s9, 1)
-    V.wait_ge(sem.s9, 1)
-    for i, (a, b) in enumerate(PARTS):
-        V.tensor_scalar(T.ro[:, a // 16:b // 16], T.s9[:, G * (a // 16) + N:G * (b // 16):G], float(ZERO), float(a), mn,
-                        AluOpType.subtract).then_inc(sem["ro%d" % i], 1)
-    V.tensor_copy(T.land[:, me].bitcast(dt.uint32),
-                  T.q[:].bitcast(dt.uint32).indirect(T.so[:, 8 * r:8 * r + 8])).then_inc(sem.ownc, 1)
+    for k, (o, a, b) in enumerate(PIECES):
+        bank, b = 512 * (k % BANKS), max(b, a + 128)
+        need(P, ["wq%d" % o] + [n % i for i, (c, d) in enumerate(PARTS) if c < b and a < d for n in ("as%d", "ac%d")])
+        if k >= BANKS:
+            need(P, ["y%d" % (k - BANKS)])
+        P.matmul_mx(T.ps[:, bank:bank + b - a], T.wq[:, 128 * o:128 * o + 128], T.wqs[:, 128 * o:128 * o + 128],
+                    T.pk[:, a:b], T.pks[:, a:b], True, True).then_inc(sem["m%d" % k], 1)
+
     Y.wait_ge(sem.lb0, 1)
     Y.wait_ge(sem.lb, 1)
     Y.dma_start(T.ln[:], T.lb[0:1, 0:9]).then_inc(sem.lnst, 16)
-
-    nc, ns = [0] * len(PARTS), [0] * len(PARTS)
-    for s in others:
-        for scales, ks, e in calls_of(topo, cores, s):
-            (ns if scales else nc)[part_of(s)] += len(e.get(r, []))
-    for q in (V, A):
-        q.wait_ge(sem.zq, 1)
-    V.wait_ge(sem.ownc, 1)
-    A.wait_ge(sem.owns, 1)
-    for i, (a, b) in enumerate(PARTS):
-        for q, name, n in ((V, "arrc%d", nc[i]), (A, "arrs%d", ns[i])):
-            q.wait_ge(sem["ro%d" % i], 1)
-            if n:
-                q.wait_ge(sem[name % i], n)
-        at = T.ro[:, a // 16:b // 16]
-        V.tensor_copy(T.pk[:, a:b].bitcast(dt.uint32),
-                      T.land[:, a:ZERO + 128].bitcast(dt.uint32).indirect(at)).then_inc(sem["ac%d" % i], 1)
-        A.activation(T.pks[:, a:b], T.lands[:, a:ZERO + 128].indirect(at), copy).then_inc(sem["as%d" % i], 1)
-
-    quantise_w(2)
-    waited = set()
-    for k, (o, a, b, by) in enumerate(PIECES):
-        bank = 512 * (k % BANKS)
-        need = ["wq%d" % max(i for i, c in enumerate(WQ_CUTS) if c <= o)]
-        need += [n % i for i, (c, d) in enumerate(PARTS) if c < b and a < d for n in ("ac%d", "as%d")]
-        for n in need:
-            if n not in waited:
-                waited.add(n)
-                P.wait_ge(sem[n], 1)
-        if k >= BANKS:
-            P.wait_ge(sem["y%d" % (k - BANKS)], 1)
-        P.matmul_mx(T.ps[:, bank:bank + b - a], T.wq[:, 128 * o:128 * o + 128], T.wqs[:, 128 * o:128 * o + 128],
-                    T.pk[:, a:b], T.pks[:, a:b], True, True).then_inc(sem["m%d" % k], 1)
-        out, src = T.yo[:, S_COLS * o + a:S_COLS * o + b], T.ps[:, bank:bank + b - a]
-        q = V if by == "V" else A
-        q.wait_ge(sem["m%d" % k], 1)
-        (V.tensor_copy(out, src) if q is V else A.activation(out, src, copy)).then_inc(sem["y%d" % k], 1)
-
     for ks in STORES:
         for k in ks:
             Y.wait_ge(sem["y%d" % k], 1)
-        a = S_COLS * PIECES[ks[0]][0] + PIECES[ks[0]][1]
-        b = S_COLS * PIECES[ks[-1]][0] + PIECES[ks[-1]][2]
+        a = min(S_COLS * PIECES[k][0] + PIECES[k][1] for k in ks)
+        b = max(S_COLS * PIECES[k][0] + PIECES[k][2] for k in ks)
         Y.dma_start(T.y[:, a:b], T.yo[:, a:b]).then_inc(sem.yst, 16)
 
     Y.wait_ge(sem.lnst, 16)

from concourse.bass import DstId, RemoteDMATransfer
from concourse.mybir import dt, AluOpType, ActivationFunctionType

N, T_COLS, CAPP, S_COLS, O = 8, 512, 128, 512, 4
GMAX = N + 1
WIN = (N + 1) * CAPP
FAR = 4096.0
X_CUTS = [0, 128, 256, 384, 512]
EARLY = 3
W_LOADS = [[0, 1], [2], [3]]
GROUPS = ["ffn", "fn", "fn"]
SWAP = True
BETWEEN = [1]
S0_TWO = False
S0_PAD = False
JOIN0 = False
W_AHEAD = 1
DEAL = {}
ALLB, LAG, WPRE = False, 0, False
AHEAD = []
ORDER = ["s0", "c0", "c1", "s1", "c2"]
TURN = -1
SHIFT = 0
CALM = 0
CALM_GROUPS, CALM_ORDER = ["ffff", "nnn"], ["c0", "s1", "c1"]
SEGMENTS = [[0, 1], [2], [3, 4], [5, 6], [7]]
SEGMENTS0 = [[0], [1], [2], [3], [4], [5], [6], [7]]
OWN_DMA = True
OWN0_DMA = True
GROUPS0 = ["ffn", "fn", "fn"]
FIRST, FIRST_FROM = False, 3
FIRST_ORDER = ["c0", "s0", "c1", "s1", "c2"]
HEAD = "q0 s q1 l"
X_BY_A = [0]
MID = {}
PARTS = [(384, 512), (192, 384), (0, 192)]
HALVES = [(256, 512), (0, 256)]
BANKS = 8
PIECES = [(0, 384, 512), (1, 384, 512), (0, 192, 384), (1, 192, 384), (0, 0, 192), (1, 0, 192),
          (2, 0, 288), (2, 288, 512), (3, 0, 320), (3, 320, 512)]
STORES = [[0], [1], [2], [3], [4], [5], [6, 7], [8, 9]]
TAIL_V = "o0 l0 t0 h0 h1 r0 r1 w0 w1 c0 c1 c2 w2 w3 y4 y5 y7 y9"
TAIL_V0 = "o0 l0 t0 h0 h1 r0 r1 w0 w1 c0 c1 c2 w2 w3 y4 y5 y7 y9"
TAIL_A = "o0 s0 s1 s2 y0 y1 y2 y3 y6 y8"

SCRATCH = {
    "xt": ("sbuf", [128, 4 * T_COLS], "bfloat16"),
    "wt": ("sbuf", [128, 512 * O], "bfloat16"),
    "zt": ("sbuf", [128, 512], "bfloat16"),
    "q": ("sbuf", [128, T_COLS], "float8_e4m3fn_x4"),
    "qs": ("sbuf", [128, T_COLS], "uint8"),
    "slot": ("sbuf", [128, N * CAPP], "float8_e4m3fn_x4"),
    "slots": ("sbuf", [128, N * CAPP], "uint8"),
    "land": ("sbuf", [128, WIN], "float8_e4m3fn_x4"),
    "lands": ("sbuf", [128, WIN], "uint8"),
    "wq": ("sbuf", [128, 128 * O], "float8_e4m3fn_x4"),
    "wqs": ("sbuf", [128, 128 * O], "uint8"),
    "pk": ("sbuf", [128, S_COLS + 128], "float8_e4m3fn_x4"),
    "pks": ("sbuf", [128, S_COLS + 128], "uint8"),
    "yo": ("sbuf", [128, O * S_COLS], "float32"),
    "ps": ("psum", [128, 512 * BANKS], "float32"),
    "cn1": ("sbuf", [128, 16], "int32"),
    "cnb": ("sbuf", [128, 72], "int32"),
    "pi": ("sbuf", [128, 8], "int32"),
    "pm": ("sbuf", [128, 8], "int32"),
    "p0": ("sbuf", [128, 8], "float32"),
    "bi": ("sbuf", [128, 32], "int32"),
    "inc": ("sbuf", [128, 64], "float32"),
    "sc": ("sbuf", [128, 64], "float32"),
    "so": ("sbuf", [128, 64], "uint16"),
    "cg": ("sbuf", [128, 4 * N], "int32"),
    "back": ("sbuf", [128, 8], "float32"),
    "mf": ("sbuf", [128, 8], "float32"),
    "lb": ("sbuf", [128, 16], "float32"),
    "ar": ("sbuf", [128, 32], "float16"),
    "keep": ("sbuf", [128, 32 * GMAX], "float16"),
    "t9": ("sbuf", [128, 32 * GMAX], "float16"),
    "s9": ("sbuf", [128, 32 * GMAX], "float16"),
    "ro": ("sbuf", [128, 32], "uint16"),
}
SEMAPHORES = (["cn", "cgot", "sent", "pi", "bi", "zt", "zq", "zp", "incm", "cown", "wgo", "lb0", "pm", "p0", "bc", "i1", "cz",
               "sc", "so", "oc", "os_", "mf", "lb", "k1", "k0", "k2", "back", "ar", "t0", "t9", "lnst", "yst"]
              + [n % i for n in ("arrc%d", "arrs%d", "h%d", "r%d", "x%d", "q%d", "w%d", "wq%d", "pc%d", "ps%d", "ac%d",
                                 "as%d") for i in range(5)]
              + ["m%d" % i for i in range(16)] + ["y%d" % i for i in range(16)])


def groups_of(topo, cores, r):
    mine = [d for d in range(N) if topo.die(cores[d]) == topo.die(cores[r])]
    far = [d for d in range(N) if d not in mine]
    i = mine.index(r)
    left = {"f": [far[(TURN * i + k + SHIFT) % len(far)] for k in range(len(far))],
            "n": [mine[(i + k) % len(mine)] for k in range(1, len(mine))]}
    if SWAP:
        if 0 in far:
            far = far[:1] + far[-1:] + far[1:-1]
        left["f"] = [far[k ^ i ^ SHIFT] for k in range(len(far))]
    if FIRST and r >= FIRST_FROM:
        late = [d for d in left["f"] + left["n"] if d >= EARLY]
        early = [d for d in range(EARLY) if d != r]
        return [early, late[:len(late) - 2], late[-2:]]
    if AHEAD:
        far, near = ([d for d in left[c] if d not in AHEAD] for c in "fn")
        pairs = [[far.pop(), near.pop()] for k in range(2)]
        return [[d for d in AHEAD if d != r], far + near] + pairs[::-1]
    return [[left[c].pop(0) for c in grp] for grp in (GROUPS if r else GROUPS0)]


def split(es, k):
    size = [1] * k
    while sum(size) + min(size) <= len(es):
        size[size.index(min(size))] *= 2
    at = [sum(size[:i]) for i in range(k + 1)]
    return [es[x:y] for x, y in zip(at, at[1:])]


def calls_of(topo, cores, r):
    others = [d for d in range(N) if d != r]
    e = topo.engines(cores[r], cores[others[0]])
    gs = groups_of(topo, cores, r)
    early = EARLY if r >= CALM else 0
    dests = {"n": others, "s0": [d for d in others if d < early], "s1": [d for d in others if d >= early]}
    if JOIN0 and not r:
        dests.update({"s0": others[:3], "s1": others[3:]})
    if S0_PAD:
        dests.update({"s0": others[:3], "s1": others[3:]})
    dests.update({"c%d" % k: grp for k, grp in enumerate(gs)})
    a, b = e[0::2], e[1::2]
    out = []
    for name in ["n"] + (FIRST_ORDER if FIRST and r >= FIRST_FROM else ORDER):
        far = [d for d in dests[name] if topo.die(cores[d]) != topo.die(cores[r])]
        near = [d for d in dests[name] if d not in far]
        k = len(far + near)
        if not k:
            continue
        if name[0] == "c" and far and near and k != 4:
            cut = split(a, len(far)) + split(b, len(near))
        elif name == "s0" and S0_TWO:
            cut = split(b, 2)
        elif name == "s1" and S0_TWO:
            light, rest = split(a, 2)
            cut = split(b, 2) + [rest] + split(light, 2)
        elif name[0] == "s" and k % 2:
            cut = split(b, k // 2 + 1) + split(a, k // 2)
        else:
            cut = split(a + b, k)
        if name + str(k) in DEAL:
            quarter = dict(zip("ABCD", split(a, 2) + split(b, 2)))
            half = dict(zip("abcdefgh", split(a, 4) + split(b, 4)))
            cut = [sum([quarter.get(x) or half[x] for x in w], []) for w in DEAL[name + str(k)].split()]
        out.append((name, dict(zip(far + near, cut))))
    return out


def segments(d):
    return SEGMENTS if d else SEGMENTS0


def slot_of(s, d):
    seg = [x for x in segments(d) if s in x][0]
    return CAPP * (N - seg[-1] + seg.index(s))


def window(a, d):
    return CAPP * (N + 1 - [x for x in segments(d) if a // CAPP in x][0][0])


def part_of(s, d):
    return min(i for i, (a, b) in enumerate(PARTS) if slot_of(s, d) < window(a, d))


def bits(es):
    return sum(1 << e for e in es)


def runs(group):
    out = []
    for d in sorted(group):
        if out and out[-1][1] == d:
            out[-1][1] = d + 1
        else:
            out.append([d, d + 1])
    return out


def rank_program(g, core, T, topo):
    r = T.rank_of(core)
    if r is None:
        return
    cores = list(T.cores)
    others = [s for s in range(N) if s != r]
    V, A, P, Y, sem = g.vector, g.scalar, g.tensor, g.sync, T.sem
    copy = ActivationFunctionType.Copy
    add, mx, mn, mul = AluOpType.add, AluOpType.max, AluOpType.min, AluOpType.mult
    calls = calls_of(topo, cores, r)
    sent = [0]
    segs = segments(r)
    G = len(segs) + 1
    a0 = segs[0][-1]
    first = 0 if [r, r + 1] in SEGMENTS else 1
    low = 0 if [r, r + 1] in SEGMENTS0 else 1

    def at(d):
        return slice(slot_of(r, d), slot_of(r, d) + CAPP)

    narrow = any(b - a < 128 for o, a, b in PIECES)
    waited = set()

    def need(q, names):
        for n in names:
            key = ([q is x for x in (V, A, P)].index(True), n)
            if key not in waited:
                waited.add(key)
                q.wait_ge(sem[n], 1)

    def send(items):
        out = []
        for d, es, src, dst, rsem in items:
            rid, pid, _ = topo.addr(cores[d])
            sent[0] += len(es)
            out.append(RemoteDMATransfer(dst_ids=[DstId(rid=rid, pnc=pid)], dma_engine_mask=bits(es), remote_sem=rsem,
                                         srcs=[src], dsts=[dst]))
        g.remote_dma_fused(out, local_sem=sem.sent)

    def load_w(tiles):
        a, b = tiles[0], tiles[-1] + 1
        Y.dma_start(T.wt[:, 512 * a:512 * b], T.w[:, 512 * a:512 * b]).then_inc(sem["w%d" % a], 16)

    def move(q, out, src):
        return V.tensor_copy(out, src) if q is V else A.activation(out, src, copy)

    Y.dma_start(T.cn1[0:1, 0:16], T.cn[:]).then_inc(sem.cn, 16)
    for k, (a, b) in enumerate(zip(X_CUTS, X_CUTS[1:])):
        (A if k in X_BY_A else Y).dma_start(T.xt[:, 4 * a:4 * b], T.x[:, 4 * a:4 * b]).then_inc(sem["x%d" % k], 16)
    for tiles in W_LOADS[:W_AHEAD]:
        load_w(tiles)

    g.iota(T.pi[:, 0:1], [[1, 1]], 0, 1).then_inc(sem.pi, 1)
    g.iota(T.bi[:], [[16, 32]], 0, 0).then_inc(sem.bi, 1)
    V.memset(T.inc[:], 16.0).then_inc(sem.incm, 1)
    V.memset(T.cnb[:], 0).then_inc(sem.cz, 1)
    V.memset(T.keep[:, 0:32 * G], 0.0).then_inc(sem.k1, 1)
    V.wait_ge(sem.pi, 1)
    V.tensor_scalar(T.pm[:, 0:1], T.pi[:, 0:1], 15, None, AluOpType.bitwise_and).then_inc(sem.pm, 1)
    V.memset(T.zt[:], 0.0).then_inc(sem.zt, 1)
    V.wait_ge(sem.pm, 1)
    V.tensor_scalar(T.p0[:, 0:1], T.pm[:, 0:1], -16.0, None, add).then_inc(sem.p0, 1)
    V.memset(T.t9[:, G - 1:32 * G:G], FAR).then_inc(sem.t0, 1)

    def fill(buf, x, z, value):
        return A.activation(buf[:, x:z], T.inc[:, 1:1 + z - x], copy, scale=value / 16.0)

    A.wait_ge(sem.incm, 1)
    jumps = T.inc[:, 8 * first:64:8]
    A.activation(jumps, jumps, copy, scale=1.0 - CAPP / 16.0).then_inc(sem.i1, 1)
    fill(T.lb, 0, 1, 0.0).then_inc(sem.lb0, 1)
    back = [0] * N
    for x, z in zip(segs, segs[1:]):
        back[z[-1] - 1] = slot_of(z[-1], r) - slot_of(x[-1], r)
    cuts = [j for j in range(a0, N - 1) if j == a0 or back[j] != back[j - 1]] + [N - 1]
    for x, z in zip(cuts, cuts[1:]):
        fill(T.back, x, z, float(back[x])).then_inc(sem.back, 1)
    V.wait_ge(sem.k1, 1)
    V.memset(T.keep[:, 0:32 * G:G], FAR).then_inc(sem.k0, 1)
    V.wait_ge(sem.bi, 1)
    V.wait_ge(sem.p0, 1)
    V.tensor_scalar(T.ar[:], T.bi[:], T.p0[:, 0:1], 16.0, add, add).then_inc(sem.ar, 1)
    V.tensor_scalar(T.keep[:, G - 1:32 * G:G], T.bi[:], T.p0[:, 0:1], 16.0, add, add).then_inc(sem.k2, 1)
    V.wait_ge(sem.zt, 1)
    V.quantize_mx(T.land[:, 0:CAPP], T.lands[:, 0:CAPP], T.zt[:]).then_inc(sem.zq, 1)
    if narrow:
        V.quantize_mx(T.pk[:, S_COLS:], T.pks[:, S_COLS:], T.zt[:]).then_inc(sem.zp, 1)
        need(P, ["zp"])

    def count(d):
        return T.cnb[:, 8 * (first + d):8 * (first + d) + 1]

    g.wait_ge(sem.cz, 1)
    g.wait_ge(sem.cn, 16)
    g.partition_broadcast(T.cnb[:, 8 * first:8 * (first + N):8], T.cn1[0:1, 0:N], 128).then_inc(sem.bc, 1)
    g.wait_ge(sem.bc, 1)
    e = calls[0][1]
    send([(d, e[d], count(d), T.cg[:, 4 * r:4 * r + 1], sem.cgot) for d in e])
    if OWN_DMA:
        Y.wait_ge(sem.bc, 1)
        Y.dma_start(T.cg[:, 4 * r:4 * r + 1], count(r)).then_inc(sem.cown, 16)
    if OWN0_DMA and r < low:
        Y.wait_ge(sem.q0, 1)
        Y.dma_start(T.lands[:, at(r)], T.qs[:, 0:CAPP]).then_inc(sem.os_, 16)
        Y.dma_start(T.land[:, at(r)].bitcast(dt.uint8), T.q[:, 0:CAPP].bitcast(dt.uint8)).then_inc(sem.oc, 16)

    def quantise_x(k):
        a, b = X_CUTS[k], X_CUTS[k + 1]
        V.wait_ge(sem["x%d" % k], 16)
        V.quantize_mx(T.q[:, a:b], T.qs[:, a:b], T.xt[:, 4 * a:4 * b]).then_inc(sem["q%d" % k], 1)

    for word in HEAD.split():
        if word == "s":
            need(V, ["bc", "i1"])
            V.tensor_tensor_scan(T.sc[:], T.cnb[:, 0:64], T.inc[:], T.p0[:, 0:1], add, add).then_inc(sem.sc, 1)
        elif word == "l":
            V.wait_ge(sem.sc, 1)
            V.tensor_scalar(T.so[:], T.sc[:], float(T_COLS - 1), None, mn).then_inc(sem.so, 1)
        else:
            quantise_x(int(word[1:]))

    call_of = {(name[0], d): name for name, deal in calls for d in deal}
    picks = {name: 0 for name, deal in calls}

    def pick(kind, a, b, out=None, done=None):
        w = min(T_COLS, CAPP * b)
        q = V if kind == "c" else A
        need(q, ["so"] + ["q%d" % k for k, c in enumerate(X_CUTS[:-1]) if c < w])
        if done is None:
            done = "p" + call_of[kind, a]
            picks[call_of[kind, a]] += 1
        if out is None:
            out = (T.slot if kind == "c" else T.slots)[:, 128 * a:128 * b]
        win = T.qs[:, 0:w]
        if kind == "c":
            out, win = out.bitcast(dt.uint32), T.q[:, 0:w].bitcast(dt.uint32)
        move(q, out, win.indirect(T.so[:, 8 * a:8 * b])).then_inc(sem[done], 1)

    landed = {(k, i): 0 for k in "cs" for i in range(len(PARTS))}
    for s in others:
        for name, e in calls_of(topo, cores, s)[1:]:
            landed[name[0], part_of(s, r)] += len(e.get(r, []))
    cg = T.cg[:, 0:4 * N:4]

    def step(q, kind, i):
        if kind == "o":
            if r >= low:
                pick(*(("c", r, r + 1, T.land[:, at(r)], "oc") if q is V else
                       ("s", r, r + 1, T.lands[:, at(r)], "os_")))
            elif q is V and not OWN0_DMA:
                V.quantize_mx(T.land[:, at(r)], T.lands[:, at(r)], T.xt[:, 0:4 * CAPP]).then_inc(sem.oc, 1)
        elif kind == "w":
            if i in [tiles[0] for tiles in W_LOADS]:
                V.wait_ge(sem["w%d" % i], 16)
            V.quantize_mx(T.wq[:, 128 * i:128 * i + 128], T.wqs[:, 128 * i:128 * i + 128],
                          T.wt[:, 512 * i:512 * i + 512]).then_inc(sem["wq%d" % i], 1)
        elif kind == "n":
            if not OWN_DMA:
                V.tensor_copy(T.cg[:, 4 * r:4 * r + 1], count(r)).then_inc(sem.cown, 1)
        elif kind == "l":
            V.wait_ge(sem.cown, 16 if OWN_DMA else 1)
            V.wait_ge(sem.cgot, sum(len(calls_of(topo, cores, s)[0][1][r]) for s in others))
            V.tensor_tensor_scan(T.lb[:, 1:9], cg, cg, 0.0, add, mx).then_inc(sem.lb, 1)
            V.wait_ge(sem.back, len(cuts) - 1)
            V.tensor_tensor_scan(T.mf[:, a0:N - 1], T.back[:, a0:N - 1], T.cg[:, 4 * a0:4 * (N - 1):4], 0.0, add,
                                 AluOpType.subtract).then_inc(sem.mf, 1)
        elif kind == "t":
            need(V, ["ar", "lb"])
            V.tensor_scalar(T.t9[:, G - 2:32 * G:G], T.ar[:], T.lb[:, N:N + 1], -FAR, AluOpType.is_ge,
                            mul).then_inc(sem.t9, 1)
            need(V, ["mf"])
            for k, x in enumerate(segs[1:]):
                V.tensor_scalar(T.t9[:, k:32 * G:G], T.ar[:], T.lb[:, x[0]:x[0] + 1], T.mf[:, x[-1] - 1:x[-1]],
                                AluOpType.is_ge, mul).then_inc(sem.t9, 1)
        elif kind == "h":
            if i == 0:
                need(V, ["k0", "k2", "t0"])
                V.wait_ge(sem.t9, G - 1)
            h = slice(G * (HALVES[i][0] // 16), G * (HALVES[i][1] // 16))
            V.tensor_tensor_scan(T.s9[:, h], T.keep[:, h], T.t9[:, h], 0.0, add, mn).then_inc(sem["h%d" % i], 1)
        elif kind == "r":
            a, b = HALVES[i][0] // 16, HALVES[i][1] // 16
            need(V, ["h%d" % i, "lb0"])
            V.tensor_scalar(T.ro[:, a:b], T.s9[:, G * a + G - 1:G * b:G], T.lb[:, a0:a0 + 1], float(slot_of(a0, r)),
                            AluOpType.subtract, add).then_inc(sem["r%d" % i], 1)
        elif kind == "y":
            o, a, b = PIECES[i]
            bank = 512 * (i % BANKS)
            need(q, ["m%d" % i])
            move(q, T.yo[:, S_COLS * o + a:S_COLS * o + b], T.ps[:, bank:bank + b - a]).then_inc(sem["y%d" % i], 1)
        else:
            a, b = PARTS[i]
            need(q, ["zq"] + ["r%d" % k for k, (c, d) in enumerate(HALVES) if c < b and a < d])
            if part_of(r, r) <= i:
                if r < low and OWN0_DMA:
                    q.wait_ge(sem["oc" if kind == "c" else "os_"], 16)
                else:
                    need(q, ["oc" if kind == "c" or r < low else "os_"])
            if landed[kind, i]:
                q.wait_ge(sem["arr%s%d" % (kind, i)], landed[kind, i])
            w = window(a, r)
            out, win = T.pks[:, a:b], T.lands[:, 0:w]
            if kind == "c":
                out, win = T.pk[:, a:b].bitcast(dt.uint32), T.land[:, 0:w].bitcast(dt.uint32)
            move(q, out, win.indirect(T.ro[:, a // 16:b // 16])).then_inc(sem["a%s%d" % (kind, i)], 1)

    def steps(q, words):
        for word in words:
            step(q, word[0], int(word[1:]))

    pairs = []
    early = EARLY if r >= CALM else 0
    mid = MID.get(r, {})
    for k in range(1, len(X_CUTS) - 1):
        if "q%d" % k not in HEAD:
            quantise_x(k)
        allb = FIRST and r >= FIRST_FROM
        for d in ([1, 2] if allb else BETWEEN):
            group = dict(calls)["c0"]
            if (d in group and 0 not in group or allb and d != r) and CAPP * (d + 1) == X_CUTS[k + LAG]:
                pick("c", d, d + 1)
                pairs.append((d, d + 1))
    for name, deal in calls:
        if name[0] == "c":
            steps(V, mid.get(name, "").split())
            rest = [d for d in deal if d >= low and (d, d + 1) not in pairs]
            alone = early if r or not JOIN0 else 2
            for a, b in [(d, d + 1) for d in rest if d < alone] + runs([d for d in rest if d >= alone]):
                pick("c", a, b)
                pairs.append((a, b))
    for a, b in sorted(pairs, key=lambda p: min(p[0], EARLY + S0_PAD)):
        pick("s", a, b)

    g.wait_ge(sem.q0, 1)
    for name, e in calls[1:]:
        if picks[name]:
            g.wait_ge(sem["p" + name], picks[name])
        if WPRE and name == calls[-1][0]:
            g.sem_inc(sem.wgo, 1)
        if name[0] == "s":
            send([(d, e[d], (T.slots if d >= low else T.qs)[:, 128 * d:128 * d + 128], T.lands[:, at(d)],
                   sem["arrs%d" % part_of(r, d)]) for d in e])
        else:
            send([(d, e[d], (T.slot if d >= low else T.q)[:, 128 * d:128 * d + 128].bitcast(dt.uint8),
                   T.land[:, at(d)].bitcast(dt.uint8), sem["arrc%d" % part_of(r, d)]) for d in e])
    if not WPRE:
        g.sem_inc(sem.wgo, 1)
    Y.wait_ge(sem.wgo, 1)
    for tiles in W_LOADS[W_AHEAD:]:
        load_w(tiles)

    done = " ".join(mid.values()).split()
    steps(V, [word for word in (TAIL_V if r else TAIL_V0).split() if word not in done])
    steps(A, TAIL_A.split())

    for k, (o, a, b) in enumerate(PIECES):
        bank, b = 512 * (k % BANKS), max(b, a + 128)
        need(P, ["wq%d" % o] + [n % i for i, (c, d) in enumerate(PARTS) if c < b and a < d for n in ("as%d", "ac%d")])
        if k >= BANKS:
            need(P, ["y%d" % (k - BANKS)])
        P.matmul_mx(T.ps[:, bank:bank + b - a], T.wq[:, 128 * o:128 * o + 128], T.wqs[:, 128 * o:128 * o + 128],
                    T.pk[:, a:b], T.pks[:, a:b], True, True).then_inc(sem["m%d" % k], 1)

    Y.wait_ge(sem.lb0, 1)
    Y.wait_ge(sem.lb, 1)
    Y.dma_start(T.ln[:], T.lb[0:1, 0:9]).then_inc(sem.lnst, 16)
    for ks in STORES:
        for k in ks:
            Y.wait_ge(sem["y%d" % k], 1)
        a = min(S_COLS * PIECES[k][0] + PIECES[k][1] for k in ks)
        b = max(S_COLS * PIECES[k][0] + PIECES[k][2] for k in ks)
        Y.dma_start(T.y[:, a:b], T.yo[:, a:b]).then_inc(sem.yst, 16)

    Y.wait_ge(sem.lnst, 16)
    Y.wait_ge(sem.yst, 16 * len(STORES))
    g.wait_ge(sem.sent, sent[0])
